import numpy as np
import ml_dtypes


def mxq(x, axis, fmt="e4m3"):
    dtype, down = {"e4m3": (ml_dtypes.float8_e4m3fn, 7), "e5m2": (ml_dtypes.float8_e5m2, 14)}[fmt]
    v = np.moveaxis(np.asarray(x, np.float32).astype(ml_dtypes.bfloat16).astype(np.float64), axis, -1)
    blocks = v.reshape(v.shape[:-1] + (-1, 32))
    amax = np.abs(blocks).max(-1, keepdims=True)
    byte = np.maximum(np.where(amax > 0, np.frexp(amax)[1] - 1 + 127, 0) - down, 1)
    scale = np.exp2(byte - 127.0)
    codes = (blocks / scale).astype(np.float32).astype(dtype).astype(np.float64)
    return np.moveaxis((codes * scale).reshape(v.shape), -1, axis)


WIDE = False


def mx_kscale(k):
    if not WIDE:
        return np.ones(k)
    levels = np.array([10, -10, 5, -5, 0])
    if k % 512:
        return np.exp2(np.random.permutation(np.resize(levels, k // 32))).repeat(32)
    a = np.empty((k // 512, 16))
    for p in range(k // 512):
        a[p, :8] = np.random.permutation(np.resize(levels, 8))
        for g in range(8):
            far = levels[np.abs(levels - a[p, g]) >= 10]
            a[p, g + 8] = far[np.random.randint(len(far))]
    return np.exp2(a.ravel()).repeat(32)


def f64(x):
    return np.asarray(x).astype(np.float64)


def striped8(idx):
    return np.concatenate([v.reshape(-1, 16).T for v in idx]).astype(np.uint16)


def unstriped8(offs):
    return np.stack([offs[16 * g:16 * g + 16].T.reshape(-1) for g in range(8)]).astype(np.int64)


E2M1 = np.array([0.0, 0.5, 1.0, 1.5, 2.0, 3.0, 4.0, 6.0, -0.0, -0.5, -1.0, -1.5, -2.0, -3.0, -4.0, -6.0])


def pack_weight(w, fmt):
    k, n = w.shape
    w = f64(np.asarray(w, np.float32).astype(ml_dtypes.bfloat16)).reshape(k // 32, 32, n)
    amax = np.abs(w).max(1)
    if fmt == "e4m3":
        byte = np.frexp(amax)[1] - 1 + 127 - 7
    else:
        mant, ex = np.frexp(amax / 6.0)
        byte = np.where(mant > 0.5, ex, ex - 1) + 127
    byte = np.clip(np.where(amax > 0, byte, 1), 1, 254)
    scaled = (w * np.exp2(127.0 - byte)[:, None, :]).reshape(k, n).astype(np.float32)
    by_word = np.ascontiguousarray(scaled.reshape(k // 512, 128, 4, n).transpose(0, 1, 3, 2))
    if fmt == "e4m3":
        words = by_word.astype(ml_dtypes.float8_e4m3fn).view(np.uint8)
    else:
        c = by_word.astype(ml_dtypes.float4_e2m1fn).view(np.uint8) & 0xF
        words = (c[..., 0::2] | (c[..., 1::2] << 4)).reshape(k // 512, 128, 2 * n)
    return np.ascontiguousarray(words), np.ascontiguousarray(byte.astype(np.uint8).reshape(k // 512, 16, n))


def unpack_weight(words, scales, fmt):
    g, _, n = scales.shape
    words = np.ascontiguousarray(words).reshape(g, 128, n, -1)
    if fmt == "e4m3":
        vals = words.view(ml_dtypes.float8_e4m3fn).astype(np.float64)
    else:
        nib = np.empty((g, 128, n, 4), np.uint8)
        nib[..., 0::2] = words & 0xF
        nib[..., 1::2] = words >> 4
        vals = E2M1[nib]
    vals = vals * np.repeat(np.exp2(scales.astype(np.float64) - 127.0), 8, axis=1)[..., None]
    return vals.transpose(0, 1, 3, 2).reshape(g * 512, n)


def silu(v):
    return v / (1.0 + np.exp(-np.maximum(v, -700.0)))


K, M, T, S = 2048, 512, 4096, 2048


def setup_inputs():
    n = np.random.standard_normal
    s = mx_kscale(K)[:, None]
    p_w = pack_weight(n((K, M)) / np.sqrt(K) / s, "e2m1")
    return {
        "x": (n((K, S)) * s).astype(np.float32),
        "w_words": p_w[0],
        "w_scales": p_w[1],
        "b": (0.3 * n(512)).astype(np.float32),
        "wgo": np.repeat(np.random.uniform(0.5, 2.0, (8, S)), 16, axis=0).astype(np.float32),
        "offs": striped8(np.stack([np.random.permutation(T)[:S] for _ in range(8)])),
    }


def reference(x, w_words, w_scales, b, wgo, offs):
    x_ = mxq(f64(x), 0, "e4m3")
    w_ = unpack_weight(w_words, w_scales, "e2m1")
    y = w_.T @ x_
    place = unstriped8(offs)[np.arange(M) % 128 // 16]
    out = np.zeros((M, T))
    out[np.arange(M)[:, None], place] = f64(wgo)[np.arange(M) % 128] * (silu(y + f64(b)[:, None]))
    return out

@@ -1,0 +1,159 @@
+from contextlib import ExitStack
+
+import concourse.mybir as mybir
+
+F32 = mybir.dt.float32
+BF16 = mybir.dt.bfloat16
+I32 = mybir.dt.int32
+U32 = mybir.dt.uint32
+U16 = mybir.dt.uint16
+U8 = mybir.dt.uint8
+E4M3 = mybir.dt.float8_e4m3fn_x4
+E2M1 = mybir.dt.float4_e2m1fn_x4
+SILU = mybir.ActivationFunctionType.Silu
+MULT = mybir.AluOpType.mult
+
+K, M, T, S = 2048, 512, 4096, 2048
+P = 128
+PASSES = K // 512
+BLOCKS = M // P
+HALF = S // 2
+BANK = 512
+FLOPS = 2 * K * M * S
+
+CHUNKS = [
+    [[(0, 1024, 640)], [(0, 1024, 640)], [(0, 1024, 640)], [(0, 512, 256), (512, 256, 128), (768, 256, 96)]],
+    [[(0, 512, 512), (512, 512, 512)], [(0, 1024, 1024)], [(0, 1024, 1024)], [(0, 512, 512), (512, 512, 64)]],
+]
+
+
+def tile_list_hscat_silu_kernel(tc, x, w_words, w_scales, b, wgo, offs, out):
+    nc = tc.nc
+    with ExitStack() as ctx:
+        keep = ctx.enter_context(tc.tile_pool(name="keep", bufs=1))
+        stage = ctx.enter_context(tc.tile_pool(name="stage", bufs=6))
+        group = ctx.enter_context(tc.tile_pool(name="group", bufs=3))
+        quant = ctx.enter_context(tc.tile_pool(name="quant", bufs=5))
+        result = ctx.enter_context(tc.tile_pool(name="result", bufs=3))
+        psum = ctx.enter_context(tc.psum_pool(name="psum", bufs=1))
+
+        offs_sb = keep.tile([P, S // 16], U16, name="offs_sb")
+        wgo_sb = keep.tile([P, S], F32, name="wgo_sb")
+        w0_sb = keep.tile([P, PASSES, 2 * P], U8, name="w0_sb", align_bytes=64)
+        w1_sb = keep.tile([P, PASSES, 2 * (M - P)], U8, name="w1_sb", align_bytes=64)
+        ws_sb = keep.tile([P, PASSES, M], U8, name="ws_sb", align_bytes=64)
+        b_sb = keep.tile([P, BLOCKS], F32, name="b_sb")
+        tiny = keep.tile([P, 8], F32, name="tiny")
+        windows = [keep.tile([P, T], F32, name=f"window{m}") for m in range(3)]
+        w_view = w_words.rearrange("a p c -> p a c")
+
+        raw = {}
+        banks = {}
+        codes = {}
+        scales = {}
+
+        def load(h, a):
+            for c0, cols, scalar_cols in CHUNKS[h][a]:
+                t = stage.tile([P, 4, cols], F32, name="raw", tag="stage")
+                lo = h * HALF + c0
+                nc.sync.dma_start(t[:], x[512 * a : 512 * a + 512, lo : lo + cols].rearrange("(p i) j -> p i j", i=4))
+                raw[h, a, c0] = t
+
+        def clear(engine, m, lo, hi):
+            engine.memset(windows[m][:, lo:hi], 0.0)
+
+        def interleave(dst, src, engine):
+            engine(dst.rearrange("p (c i) t -> p c t i", i=4), src.rearrange("p t (c i) -> p c t i", i=4))
+
+        def quantize(h, a):
+            codes[h, a] = quant.tile([P, HALF], U32, name="codes", align_bytes=64)
+            scales[h, a] = quant.tile([P, HALF], U8, name="scales", align_bytes=64)
+            for c0, cols, scalar_cols in CHUNKS[h][a]:
+                grouped = group.tile([P, cols, 4], BF16, name="grouped", align_bytes=64)
+                src = raw[h, a, c0]
+                if scalar_cols > 0:
+                    interleave(grouped[:, 0:scalar_cols, :], src[:, :, 0:scalar_cols], nc.scalar.copy)
+                if scalar_cols < cols:
+                    interleave(grouped[:, scalar_cols:cols, :], src[:, :, scalar_cols:cols], nc.vector.tensor_copy)
+                nc.vector.quantize_mx(
+                    out=codes[h, a][:, c0 : c0 + cols].bitcast(E4M3),
+                    scales=scales[h, a][:, c0 : c0 + cols],
+                    in_=grouped[:].rearrange("p c t -> p (c t)"),
+                )
+
+        def multiply(h, a, m):
+            words = w0_sb[:, a, :] if m == 0 else w1_sb[:, a, 2 * P * (m - 1) : 2 * P * m]
+            for n in range(HALF // BANK):
+                if a == 0:
+                    banks[h, m, n] = psum.tile([P, BANK], F32, name=f"bank{m}{n}")
+                nc.tensor.matmul_mx(
+                    out=banks[h, m, n][:],
+                    lhsT=words.bitcast(E2M1),
+                    lhsT_scale=ws_sb[:, a, P * m : P * (m + 1)],
+                    rhs=codes[h, a][:, n * BANK : (n + 1) * BANK].bitcast(E4M3),
+                    rhs_scale=scales[h, a][:, n * BANK : (n + 1) * BANK],
+                    start=(a == 0),
+                    stop=(a == PASSES - 1),
+                )
+
+        def place(h, m):
+            y = result.tile([P, HALF], F32, name="y")
+            for n in range(HALF // BANK):
+                nc.scalar.activation(y[:, n * BANK : (n + 1) * BANK], banks[h, m, n][:], SILU, bias=b_sb[:, m : m + 1])
+            nc.vector.tensor_tensor(
+                windows[m][:].indirect(offs_sb[:, h * HALF // 16 : (h + 1) * HALF // 16]),
+                y[:],
+                wgo_sb[:, h * HALF : (h + 1) * HALF],
+                MULT,
+            )
+
+        load(0, 0)
+        nc.vector.memset(tiny[:], 0.0)
+        nc.vector.memset(ws_sb[:].bitcast(I32), 0)
+        nc.scalar.activation(tiny[:, 0:1], tiny[:, 1:2], SILU)
+        nc.scalar.dma_start(w0_sb[:].bitcast(I32), w_view[:, :, 0 : 2 * P].bitcast(I32))
+        for q in range(4):
+            nc.scalar.dma_start(ws_sb[32 * q : 32 * q + 4, :, :].bitcast(I32), w_scales[:, 4 * q : 4 * q + 4, :].rearrange("a q n -> q a n").bitcast(I32))
+        with nc.allow_non_contiguous_dma(reason="512 bias values, one to a partition and block"):
+            nc.scalar.dma_start(b_sb[:], b.rearrange("(m p) -> p m", p=P))
+        for a in range(1, PASSES):
+            load(0, a)
+        nc.sync.dma_start(offs_sb[:], offs)
+        nc.sync.dma_start(wgo_sb[:, 0:HALF], wgo[:, 0:HALF])
+        nc.sync.dma_start(w1_sb[:].bitcast(I32), w_view[:, :, 2 * P : 2 * M].bitcast(I32))
+        clear(nc.vector, 0, 0, 2048)
+        for lo in range(0, T, 1024):
+            clear(nc.gpsimd, 2, lo, lo + 1024)
+
+        for a in range(PASSES):
+            quantize(0, a)
+            multiply(0, a, 0)
+            if a == 0:
+                clear(nc.vector, 0, 2048, 3072)
+                clear(nc.vector, 0, 3072, 4096)
+            elif a < 3:
+                clear(nc.vector, 1, 2048 * (a - 1), 2048 * (a - 1) + 1024)
+                clear(nc.vector, 1, 2048 * (a - 1) + 1024, 2048 * a)
+        load(1, 0)
+        load(1, 1)
+        nc.sync.dma_start(wgo_sb[:, HALF:S], wgo[:, HALF:S])
+        load(1, 2)
+        load(1, 3)
+        window = stage.tile([P, T], F32, name="window", tag="stage")
+        windows.append(window)
+        for lo in range(0, T, 512):
+            clear(nc.gpsimd, 3, lo, lo + 512)
+        for m in range(BLOCKS):
+            if m > 0:
+                for a in range(PASSES):
+                    multiply(0, a, m)
+            if m == BLOCKS - 1:
+                quantize(1, m)
+            place(0, m)
+            if m < BLOCKS - 1:
+                quantize(1, m)
+        for m in range(BLOCKS):
+            for a in range(PASSES):
+                multiply(1, a, m)
+            place(1, m)
+            nc.sync.dma_start(out[P * m : P * (m + 1), :], windows[m][:])

@@ -17,34 +17,32 @@ K, M, T, S = 2048, 512, 4096, 2048
 P = 128
 PASSES = K // 512
 BLOCKS = M // P
-HALF = S // 2
 BANK = 512
 FLOPS = 2 * K * M * S
 
-CHUNKS = [
-    [[(0, 1024, 640)], [(0, 1024, 640)], [(0, 1024, 640)], [(0, 512, 256), (512, 256, 128), (768, 256, 96)]],
-    [[(0, 512, 512), (512, 512, 512)], [(0, 1024, 1024)], [(0, 1024, 1024)], [(0, 512, 512), (512, 512, 64)]],
-]
+WIDTHS = [256, 256, 256, 256, 512, 512]
+STARTS = [sum(WIDTHS[:c]) for c in range(len(WIDTHS))]
+LAST = len(WIDTHS) - 1
 
 
 def tile_list_hscat_silu_kernel(tc, x, w_words, w_scales, b, wgo, offs, out):
     nc = tc.nc
     with ExitStack() as ctx:
         keep = ctx.enter_context(tc.tile_pool(name="keep", bufs=1))
-        stage = ctx.enter_context(tc.tile_pool(name="stage", bufs=6))
-        group = ctx.enter_context(tc.tile_pool(name="group", bufs=3))
-        quant = ctx.enter_context(tc.tile_pool(name="quant", bufs=5))
+        stage = ctx.enter_context(tc.tile_pool(name="stage", bufs=1))
+        group = ctx.enter_context(tc.tile_pool(name="group", bufs=5))
+        quant = ctx.enter_context(tc.tile_pool(name="quant", bufs=6))
         result = ctx.enter_context(tc.tile_pool(name="result", bufs=3))
         psum = ctx.enter_context(tc.psum_pool(name="psum", bufs=1))
 
         offs_sb = keep.tile([P, S // 16], U16, name="offs_sb")
-        wgo_sb = keep.tile([P, S], F32, name="wgo_sb")
         w0_sb = keep.tile([P, PASSES, 2 * P], U8, name="w0_sb", align_bytes=64)
         w1_sb = keep.tile([P, PASSES, 2 * (M - P)], U8, name="w1_sb", align_bytes=64)
         ws_sb = keep.tile([P, PASSES, M], U8, name="ws_sb", align_bytes=64)
         b_sb = keep.tile([P, BLOCKS], F32, name="b_sb")
         tiny = keep.tile([P, 8], F32, name="tiny")
-        windows = [keep.tile([P, T], F32, name=f"window{m}") for m in range(3)]
+        wgo_sb = keep.tile([P, S], F32, name="wgo_sb")
+        windows = [keep.tile([P, T], F32, name=f"window{m}") for m in range(BLOCKS)]
         w_view = w_words.rearrange("a p c -> p a c")
 
         raw = {}
@@ -52,108 +50,123 @@ def tile_list_hscat_silu_kernel(tc, x, w_words, w_scales, b, wgo, offs, out):
         codes = {}
         scales = {}
 
-        def load(h, a):
-            for c0, cols, scalar_cols in CHUNKS[h][a]:
-                t = stage.tile([P, 4, cols], F32, name="raw", tag="stage")
-                lo = h * HALF + c0
-                nc.sync.dma_start(t[:], x[512 * a : 512 * a + 512, lo : lo + cols].rearrange("(p i) j -> p i j", i=4))
-                raw[h, a, c0] = t
+        def load(c, a):
+            cols = WIDTHS[c]
+            t = stage.tile([P, 4, cols], F32, name="raw", tag=f"raw{cols}", bufs=16 if cols == 256 else 6)
+            nc.sync.dma_start(t[:], x[512 * a : 512 * a + 512, STARTS[c] : STARTS[c] + cols].rearrange("(p i) j -> p i j", i=4))
+            raw[c, a] = t
 
-        def clear(engine, m, lo, hi):
-            engine.memset(windows[m][:, lo:hi], 0.0)
+        def load_wgo(lo, hi):
+            nc.sync.dma_start(wgo_sb[:, lo:hi], wgo[:, lo:hi])
+
+        def clear(engine, m, cuts):
+            for lo, hi in zip(cuts[:-1], cuts[1:]):
+                engine.memset(windows[m][:, lo:hi], 0.0)
 
         def interleave(dst, src, engine):
             engine(dst.rearrange("p (c i) t -> p c t i", i=4), src.rearrange("p t (c i) -> p c t i", i=4))
 
-        def quantize(h, a):
-            codes[h, a] = quant.tile([P, HALF], U32, name="codes", align_bytes=64)
-            scales[h, a] = quant.tile([P, HALF], U8, name="scales", align_bytes=64)
-            for c0, cols, scalar_cols in CHUNKS[h][a]:
-                grouped = group.tile([P, cols, 4], BF16, name="grouped", align_bytes=64)
-                src = raw[h, a, c0]
-                if scalar_cols > 0:
-                    interleave(grouped[:, 0:scalar_cols, :], src[:, :, 0:scalar_cols], nc.scalar.copy)
-                if scalar_cols < cols:
-                    interleave(grouped[:, scalar_cols:cols, :], src[:, :, scalar_cols:cols], nc.vector.tensor_copy)
-                nc.vector.quantize_mx(
-                    out=codes[h, a][:, c0 : c0 + cols].bitcast(E4M3),
-                    scales=scales[h, a][:, c0 : c0 + cols],
-                    in_=grouped[:].rearrange("p c t -> p (c t)"),
-                )
+        def quantize(c, a):
+            cols = WIDTHS[c]
+            grouped = group.tile([P, cols, 4], BF16, name="grouped", align_bytes=64)
+            codes[c, a] = quant.tile([P, cols], U32, name="codes", align_bytes=64)
+            scales[c, a] = quant.tile([P, cols], U8, name="scales", align_bytes=64)
+            split = 96 if (c, a) == (0, PASSES - 1) else cols
+            interleave(grouped[:, 0:split, :], raw[c, a][:, :, 0:split], nc.scalar.copy)
+            if split < cols:
+                interleave(grouped[:, split:cols, :], raw[c, a][:, :, split:cols], nc.vector.tensor_copy)
+            nc.vector.quantize_mx(out=codes[c, a][:].bitcast(E4M3), scales=scales[c, a][:], in_=grouped[:].rearrange("p c t -> p (c t)"))
 
-        def multiply(h, a, m):
-            words = w0_sb[:, a, :] if m == 0 else w1_sb[:, a, 2 * P * (m - 1) : 2 * P * m]
-            for n in range(HALF // BANK):
-                if a == 0:
-                    banks[h, m, n] = psum.tile([P, BANK], F32, name=f"bank{m}{n}")
-                nc.tensor.matmul_mx(
-                    out=banks[h, m, n][:],
-                    lhsT=words.bitcast(E2M1),
-                    lhsT_scale=ws_sb[:, a, P * m : P * (m + 1)],
-                    rhs=codes[h, a][:, n * BANK : (n + 1) * BANK].bitcast(E4M3),
-                    rhs_scale=scales[h, a][:, n * BANK : (n + 1) * BANK],
-                    start=(a == 0),
-                    stop=(a == PASSES - 1),
-                )
+        def multiply(c, m):
+            cols = WIDTHS[c]
+            step = BANK if cols == BANK else P
+            banks[c, m] = psum.tile([P, BANK], F32, name=f"bank{c % 2}{m}")
+            for a in range(PASSES):
+                words = w0_sb[:, a, :] if m == 0 else w1_sb[:, a, 2 * P * (m - 1) : 2 * P * m]
+                for lo in range(0, cols, step):
+                    nc.tensor.matmul_mx(
+                        out=banks[c, m][:, lo : lo + step],
+                        lhsT=words.bitcast(E2M1),
+                        lhsT_scale=ws_sb[:, a, P * m : P * (m + 1)],
+                        rhs=codes[c, a][:, lo : lo + step].bitcast(E4M3),
+                        rhs_scale=scales[c, a][:, lo : lo + step],
+                        start=(a == 0 and lo == 0),
+                        stop=(a == PASSES - 1 and lo + step == cols),
+                    )
 
-        def place(h, m):
-            y = result.tile([P, HALF], F32, name="y")
-            for n in range(HALF // BANK):
-                nc.scalar.activation(y[:, n * BANK : (n + 1) * BANK], banks[h, m, n][:], SILU, bias=b_sb[:, m : m + 1])
-            nc.vector.tensor_tensor(
-                windows[m][:].indirect(offs_sb[:, h * HALF // 16 : (h + 1) * HALF // 16]),
-                y[:],
-                wgo_sb[:, h * HALF : (h + 1) * HALF],
-                MULT,
-            )
+        def activate(c, m, y):
+            nc.scalar.activation(y, banks[c, m][:, 0 : WIDTHS[c]], SILU, bias=b_sb[:, m : m + 1])
 
-        load(0, 0)
+        def scatter(m, lo, hi, y):
+            nc.vector.tensor_tensor(windows[m][:].indirect(offs_sb[:, lo // 16 : hi // 16]), y, wgo_sb[:, lo:hi], MULT)
+
+        def place(c, m, y):
+            activate(c, m, y)
+            scatter(m, STARTS[c], STARTS[c] + WIDTHS[c], y)
+
+        def place_now(c, m):
+            y = result.tile([P, WIDTHS[c]], F32, name="y")
+            place(c, m, y[:])
+
+        def store(m):
+            nc.sync.dma_start(out[P * m : P * (m + 1), :], windows[m][:])
+
         nc.vector.memset(tiny[:], 0.0)
-        nc.vector.memset(ws_sb[:].bitcast(I32), 0)
         nc.scalar.activation(tiny[:, 0:1], tiny[:, 1:2], SILU)
-        nc.scalar.dma_start(w0_sb[:].bitcast(I32), w_view[:, :, 0 : 2 * P].bitcast(I32))
+        load(0, 0)
         for q in range(4):
-            nc.scalar.dma_start(ws_sb[32 * q : 32 * q + 4, :, :].bitcast(I32), w_scales[:, 4 * q : 4 * q + 4, :].rearrange("a q n -> q a n").bitcast(I32))
-        with nc.allow_non_contiguous_dma(reason="512 bias values, one to a partition and block"):
-            nc.scalar.dma_start(b_sb[:], b.rearrange("(m p) -> p m", p=P))
+            nc.sync.dma_start(ws_sb[32 * q : 32 * q + 4, :, :].bitcast(I32), w_scales[:, 4 * q : 4 * q + 4, :].rearrange("a q n -> q a n").bitcast(I32))
+        nc.sync.dma_start(w0_sb[:].bitcast(I32), w_view[:, :, 0 : 2 * P].bitcast(I32))
         for a in range(1, PASSES):
             load(0, a)
+        with nc.allow_non_contiguous_dma(reason="512 bias values, one to a partition and block"):
+            nc.sync.dma_start(b_sb[:], b.rearrange("(m p) -> p m", p=P))
         nc.sync.dma_start(offs_sb[:], offs)
-        nc.sync.dma_start(wgo_sb[:, 0:HALF], wgo[:, 0:HALF])
+        load_wgo(0, 512)
         nc.sync.dma_start(w1_sb[:].bitcast(I32), w_view[:, :, 2 * P : 2 * M].bitcast(I32))
-        clear(nc.vector, 0, 0, 2048)
-        for lo in range(0, T, 1024):
-            clear(nc.gpsimd, 2, lo, lo + 1024)
-
-        for a in range(PASSES):
-            quantize(0, a)
-            multiply(0, a, 0)
-            if a == 0:
-                clear(nc.vector, 0, 2048, 3072)
-                clear(nc.vector, 0, 3072, 4096)
-            elif a < 3:
-                clear(nc.vector, 1, 2048 * (a - 1), 2048 * (a - 1) + 1024)
-                clear(nc.vector, 1, 2048 * (a - 1) + 1024, 2048 * a)
-        load(1, 0)
-        load(1, 1)
-        nc.sync.dma_start(wgo_sb[:, HALF:S], wgo[:, HALF:S])
-        load(1, 2)
-        load(1, 3)
-        window = stage.tile([P, T], F32, name="window", tag="stage")
-        windows.append(window)
-        for lo in range(0, T, 512):
-            clear(nc.gpsimd, 3, lo, lo + 512)
-        for m in range(BLOCKS):
-            if m > 0:
-                for a in range(PASSES):
-                    multiply(0, a, m)
-            if m == BLOCKS - 1:
-                quantize(1, m)
-            place(0, m)
-            if m < BLOCKS - 1:
-                quantize(1, m)
-        for m in range(BLOCKS):
+        for c in range(1, LAST + 1):
             for a in range(PASSES):
-                multiply(1, a, m)
-            place(1, m)
-            nc.sync.dma_start(out[P * m : P * (m + 1), :], windows[m][:])
+                load(c, a)
+            if c == 2:
+                load_wgo(512, 1024)
+            if c == 4:
+                load_wgo(1024, S)
+        clear(nc.vector, 0, [0, 2047, T])
+        clear(nc.gpsimd, 1, [0, T])
+        clear(nc.gpsimd, 2, list(range(0, T + 1, 512)))
+        clear(nc.gpsimd, 3, list(range(T // 2, T + 1, 512)))
+
+        def quantize_passes(c, passes):
+            for a in passes:
+                quantize(c, a)
+
+        y_tail = raw[LAST, 1][:, 2:4, :].rearrange("p i j -> p (i j)")
+        quantize_passes(0, range(PASSES))
+        clear(nc.vector, 3, [0, 511, 1024, 1535, T // 2])
+        for c in range(LAST + 1):
+            ahead = 2 if c in (LAST - 2, LAST - 1) else 0
+            for m in range(BLOCKS):
+                multiply(c, m)
+            if c < LAST:
+                quantize_passes(c + 1, range(ahead))
+            if c < LAST - 2:
+                for m in range(BLOCKS - 1):
+                    place_now(c, m)
+            elif c == LAST - 2:
+                for m in range(BLOCKS - 1):
+                    place(c, m, raw[c + 1, 1][:, m, 0 : WIDTHS[c]])
+            elif c == LAST - 1:
+                for m in range(2):
+                    place(c, m, raw[c + 1, 1][:, m, 0 : WIDTHS[c]])
+                activate(c, BLOCKS - 1, y_tail[:, 0 : WIDTHS[c]])
+            else:
+                for m in range(BLOCKS - 1):
+                    place_now(c, m)
+                    store(m)
+                activate(c, BLOCKS - 1, y_tail[:, WIDTHS[c - 1] :])
+                scatter(BLOCKS - 1, STARTS[c - 1], S, y_tail)
+                store(BLOCKS - 1)
+            if c < LAST:
+                quantize_passes(c + 1, range(ahead, PASSES))
+                held = BLOCKS - 1 if c < LAST - 1 else 2
+                place(c, held, raw[c + 1, PASSES - 1][:, 0, 0 : WIDTHS[c]])

@@ -111,6 +111,8 @@ def tile_list_hscat_silu_kernel(tc, x, w_words, w_scales, b, wgo, offs, out):
         def store(m):
             nc.sync.dma_start(out[P * m : P * (m + 1), :], windows[m][:])
 
+        with nc.allow_non_contiguous_dma(reason="512 bias values, one to a partition and block"):
+            nc.scalar.dma_start(b_sb[:], b.rearrange("(m p) -> p m", p=P))
         nc.vector.memset(tiny[:], 0.0)
         nc.scalar.activation(tiny[:, 0:1], tiny[:, 1:2], SILU)
         load(0, 0)
@@ -119,16 +121,14 @@ def tile_list_hscat_silu_kernel(tc, x, w_words, w_scales, b, wgo, offs, out):
         nc.sync.dma_start(w0_sb[:].bitcast(I32), w_view[:, :, 0 : 2 * P].bitcast(I32))
         for a in range(1, PASSES):
             load(0, a)
-        with nc.allow_non_contiguous_dma(reason="512 bias values, one to a partition and block"):
-            nc.sync.dma_start(b_sb[:], b.rearrange("(m p) -> p m", p=P))
         nc.sync.dma_start(offs_sb[:], offs)
-        load_wgo(0, 512)
+        load_wgo(0, 256)
         nc.sync.dma_start(w1_sb[:].bitcast(I32), w_view[:, :, 2 * P : 2 * M].bitcast(I32))
         for c in range(1, LAST + 1):
             for a in range(PASSES):
                 load(c, a)
-            if c == 2:
-                load_wgo(512, 1024)
+            if c == 1:
+                load_wgo(256, 1024)
             if c == 4:
                 load_wgo(1024, S)
         clear(nc.vector, 0, [0, 2047, T])
@@ -136,37 +136,34 @@ def tile_list_hscat_silu_kernel(tc, x, w_words, w_scales, b, wgo, offs, out):
         clear(nc.gpsimd, 2, list(range(0, T + 1, 512)))
         clear(nc.gpsimd, 3, list(range(T // 2, T + 1, 512)))
 
-        def quantize_passes(c, passes):
-            for a in passes:
-                quantize(c, a)
+        def lag(c, m):
+            if c == 0:
+                return m if m < BLOCKS - 1 else PASSES
+            return m + (1 if WIDTHS[c + 1] == 256 else 2)
 
-        y_tail = raw[LAST, 1][:, 2:4, :].rearrange("p i j -> p (i j)")
-        quantize_passes(0, range(PASSES))
-        clear(nc.vector, 3, [0, 511, 1024, 1535, T // 2])
-        for c in range(LAST + 1):
-            ahead = 2 if c in (LAST - 2, LAST - 1) else 0
+        held = {}
+        for c in range(LAST):
             for m in range(BLOCKS):
-                multiply(c, m)
-            if c < LAST:
-                quantize_passes(c + 1, range(ahead))
-            if c < LAST - 2:
-                for m in range(BLOCKS - 1):
-                    place_now(c, m)
-            elif c == LAST - 2:
-                for m in range(BLOCKS - 1):
-                    place(c, m, raw[c + 1, 1][:, m, 0 : WIDTHS[c]])
-            elif c == LAST - 1:
-                for m in range(2):
-                    place(c, m, raw[c + 1, 1][:, m, 0 : WIDTHS[c]])
-                activate(c, BLOCKS - 1, y_tail[:, 0 : WIDTHS[c]])
-            else:
-                for m in range(BLOCKS - 1):
-                    place_now(c, m)
-                    store(m)
-                activate(c, BLOCKS - 1, y_tail[:, WIDTHS[c - 1] :])
-                scatter(BLOCKS - 1, STARTS[c - 1], S, y_tail)
-                store(BLOCKS - 1)
-            if c < LAST:
-                quantize_passes(c + 1, range(ahead, PASSES))
-                held = BLOCKS - 1 if c < LAST - 1 else 2
-                place(c, held, raw[c + 1, PASSES - 1][:, 0, 0 : WIDTHS[c]])
+                held[PASSES * c + PASSES - 1 + lag(c, m)] = (c, m)
+        y_tail = raw[LAST, PASSES - 1][:, 2:4, :].rearrange("p i j -> p (i j)")
+
+        for step in range(PASSES * (LAST + 1)):
+            c, a = divmod(step, PASSES)
+            quantize(c, a)
+            if a == PASSES - 1:
+                if c == 0:
+                    clear(nc.vector, 3, [0, 511, 1024, 1535, T // 2])
+                for m in range(BLOCKS):
+                    multiply(c, m)
+            if step == PASSES - 1:
+                place_now(0, 0)
+            elif step in held:
+                hc, hm = held[step]
+                place(hc, hm, raw[c, a][:, 0, 0 : WIDTHS[hc]])
+        activate(LAST - 1, BLOCKS - 1, y_tail[:, 0 : WIDTHS[LAST - 1]])
+        for m in range(BLOCKS - 1):
+            place_now(LAST, m)
+            store(m)
+        activate(LAST, BLOCKS - 1, y_tail[:, WIDTHS[LAST - 1] :])
+        scatter(BLOCKS - 1, STARTS[LAST - 1], S, y_tail)
+        store(BLOCKS - 1)

@@ -64,7 +64,7 @@ def tile_list_hscat_silu_kernel(tc, x, w_words, w_scales, b, wgo, offs, out):
                 engine.memset(windows[m][:, lo:hi], 0.0)
 
         def interleave(dst, src, engine):
-            engine(dst.rearrange("p (c i) t -> p c t i", i=4), src.rearrange("p t (c i) -> p c t i", i=4))
+            engine(dst.rearrange("p (c i) t -> p c t i", i=2), src.rearrange("p t (c i) -> p c t i", i=2))
 
         def quantize(c, a):
             cols = WIDTHS[c]
@@ -139,7 +139,7 @@ def tile_list_hscat_silu_kernel(tc, x, w_words, w_scales, b, wgo, offs, out):
         def lag(c, m):
             if c == 0:
                 return m if m < BLOCKS - 1 else PASSES
-            return m + (1 if WIDTHS[c + 1] == 256 else 2)
+            return m + 1 if m < (BLOCKS - 1 if c < LAST - 1 else 2) else PASSES + (m == BLOCKS - 1 and c == LAST - 1)
 
         held = {}
         for c in range(LAST):

@@ -36,8 +36,7 @@ def tile_list_hscat_silu_kernel(tc, x, w_words, w_scales, b, wgo, offs, out):
         psum = ctx.enter_context(tc.psum_pool(name="psum", bufs=1))
 
         offs_sb = keep.tile([P, S // 16], U16, name="offs_sb")
-        w0_sb = keep.tile([P, PASSES, 2 * P], U8, name="w0_sb", align_bytes=64)
-        w1_sb = keep.tile([P, PASSES, 2 * (M - P)], U8, name="w1_sb", align_bytes=64)
+        w_sb = keep.tile([P, PASSES, 2 * M], U8, name="w_sb", align_bytes=64)
         ws_sb = keep.tile([P, PASSES, M], U8, name="ws_sb", align_bytes=64)
         b_sb = keep.tile([P, BLOCKS], F32, name="b_sb")
         tiny = keep.tile([P, 8], F32, name="tiny")
@@ -64,15 +63,16 @@ def tile_list_hscat_silu_kernel(tc, x, w_words, w_scales, b, wgo, offs, out):
                 engine.memset(windows[m][:, lo:hi], 0.0)
 
         def interleave(dst, src, engine):
-            engine(dst.rearrange("p (c i) t -> p c t i", i=2), src.rearrange("p t (c i) -> p c t i", i=2))
+            engine(dst.rearrange("p (c i) t -> p c t i", i=4), src.rearrange("p t (c i) -> p c t i", i=4))
 
         def quantize(c, a):
             cols = WIDTHS[c]
             grouped = group.tile([P, cols, 4], BF16, name="grouped", align_bytes=64)
             codes[c, a] = quant.tile([P, cols], U32, name="codes", align_bytes=64)
             scales[c, a] = quant.tile([P, cols], U8, name="scales", align_bytes=64)
-            split = 96 if (c, a) == (0, PASSES - 1) else cols
-            interleave(grouped[:, 0:split, :], raw[c, a][:, :, 0:split], nc.scalar.copy)
+            split = 96 if (c, a) == (0, PASSES - 1) else 0 if (c, a) == (LAST - 1, 1) else cols
+            if split > 0:
+                interleave(grouped[:, 0:split, :], raw[c, a][:, :, 0:split], nc.scalar.copy)
             if split < cols:
                 interleave(grouped[:, split:cols, :], raw[c, a][:, :, split:cols], nc.vector.tensor_copy)
             nc.vector.quantize_mx(out=codes[c, a][:].bitcast(E4M3), scales=scales[c, a][:], in_=grouped[:].rearrange("p c t -> p (c t)"))
@@ -82,7 +82,7 @@ def tile_list_hscat_silu_kernel(tc, x, w_words, w_scales, b, wgo, offs, out):
             step = BANK if cols == BANK else P
             banks[c, m] = psum.tile([P, BANK], F32, name=f"bank{c % 2}{m}")
             for a in range(PASSES):
-                words = w0_sb[:, a, :] if m == 0 else w1_sb[:, a, 2 * P * (m - 1) : 2 * P * m]
+                words = w_sb[:, a, 2 * P * m : 2 * P * (m + 1)]
                 for lo in range(0, cols, step):
                     nc.tensor.matmul_mx(
                         out=banks[c, m][:, lo : lo + step],
@@ -118,19 +118,18 @@ def tile_list_hscat_silu_kernel(tc, x, w_words, w_scales, b, wgo, offs, out):
         load(0, 0)
         for q in range(4):
             nc.sync.dma_start(ws_sb[32 * q : 32 * q + 4, :, :].bitcast(I32), w_scales[:, 4 * q : 4 * q + 4, :].rearrange("a q n -> q a n").bitcast(I32))
-        nc.sync.dma_start(w0_sb[:].bitcast(I32), w_view[:, :, 0 : 2 * P].bitcast(I32))
         for a in range(1, PASSES):
             load(0, a)
+        nc.sync.dma_start(w_sb[:].bitcast(I32), w_view.bitcast(I32))
         nc.sync.dma_start(offs_sb[:], offs)
         load_wgo(0, 256)
-        nc.sync.dma_start(w1_sb[:].bitcast(I32), w_view[:, :, 2 * P : 2 * M].bitcast(I32))
         for c in range(1, LAST + 1):
             for a in range(PASSES):
                 load(c, a)
             if c == 1:
                 load_wgo(256, 1024)
-            if c == 4:
-                load_wgo(1024, S)
+            if c >= LAST - 1:
+                load_wgo(STARTS[c], STARTS[c] + WIDTHS[c])
         clear(nc.vector, 0, [0, 2047, T])
         clear(nc.gpsimd, 1, [0, T])
         clear(nc.gpsimd, 2, list(range(0, T + 1, 512)))
@@ -159,7 +158,10 @@ def tile_list_hscat_silu_kernel(tc, x, w_words, w_scales, b, wgo, offs, out):
                 place_now(0, 0)
             elif step in held:
                 hc, hm = held[step]
-                place(hc, hm, raw[c, a][:, 0, 0 : WIDTHS[hc]])
+                if (c, a) == (LAST - 1, 1):
+                    place(hc, hm, raw[c, 0][:, 1, 0 : WIDTHS[hc]])
+                else:
+                    place(hc, hm, raw[c, a][:, 0, 0 : WIDTHS[hc]])
         activate(LAST - 1, BLOCKS - 1, y_tail[:, 0 : WIDTHS[LAST - 1]])
         for m in range(BLOCKS - 1):
             place_now(LAST, m)

@@ -32,11 +32,11 @@ def tile_list_hscat_silu_kernel(tc, x, w_words, w_scales, b, wgo, offs, out):
         stage = ctx.enter_context(tc.tile_pool(name="stage", bufs=1))
         group = ctx.enter_context(tc.tile_pool(name="group", bufs=5))
         quant = ctx.enter_context(tc.tile_pool(name="quant", bufs=6))
-        result = ctx.enter_context(tc.tile_pool(name="result", bufs=3))
+        result = ctx.enter_context(tc.tile_pool(name="result", bufs=1))
         psum = ctx.enter_context(tc.psum_pool(name="psum", bufs=1))
 
         offs_sb = keep.tile([P, S // 16], U16, name="offs_sb")
-        w_sb = keep.tile([P, PASSES, 2 * M], U8, name="w_sb", align_bytes=64)
+        w_sb = [keep.tile([P, PASSES, M], U8, name=f"w_sb{h}", align_bytes=64) for h in range(2)]
         ws_sb = keep.tile([P, PASSES, M], U8, name="ws_sb", align_bytes=64)
         b_sb = keep.tile([P, BLOCKS], F32, name="b_sb")
         tiny = keep.tile([P, 8], F32, name="tiny")
@@ -51,7 +51,7 @@ def tile_list_hscat_silu_kernel(tc, x, w_words, w_scales, b, wgo, offs, out):
 
         def load(c, a):
             cols = WIDTHS[c]
-            t = stage.tile([P, 4, cols], F32, name="raw", tag=f"raw{cols}", bufs=16 if cols == 256 else 6)
+            t = stage.tile([P, 4, cols], F32, name="raw", tag=f"raw{cols}", bufs=12 if cols == 256 else 8)
             nc.sync.dma_start(t[:], x[512 * a : 512 * a + 512, STARTS[c] : STARTS[c] + cols].rearrange("(p i) j -> p i j", i=4))
             raw[c, a] = t
 
@@ -70,9 +70,8 @@ def tile_list_hscat_silu_kernel(tc, x, w_words, w_scales, b, wgo, offs, out):
             grouped = group.tile([P, cols, 4], BF16, name="grouped", align_bytes=64)
             codes[c, a] = quant.tile([P, cols], U32, name="codes", align_bytes=64)
             scales[c, a] = quant.tile([P, cols], U8, name="scales", align_bytes=64)
-            split = 96 if (c, a) == (0, PASSES - 1) else 0 if (c, a) == (LAST - 1, 1) else cols
-            if split > 0:
-                interleave(grouped[:, 0:split, :], raw[c, a][:, :, 0:split], nc.scalar.copy)
+            split = 96 if (c, a) == (0, PASSES - 1) else cols
+            interleave(grouped[:, 0:split, :], raw[c, a][:, :, 0:split], nc.scalar.copy)
             if split < cols:
                 interleave(grouped[:, split:cols, :], raw[c, a][:, :, split:cols], nc.vector.tensor_copy)
             nc.vector.quantize_mx(out=codes[c, a][:].bitcast(E4M3), scales=scales[c, a][:], in_=grouped[:].rearrange("p c t -> p (c t)"))
@@ -82,7 +81,7 @@ def tile_list_hscat_silu_kernel(tc, x, w_words, w_scales, b, wgo, offs, out):
             step = BANK if cols == BANK else P
             banks[c, m] = psum.tile([P, BANK], F32, name=f"bank{c % 2}{m}")
             for a in range(PASSES):
-                words = w_sb[:, a, 2 * P * m : 2 * P * (m + 1)]
+                words = w_sb[m // 2][:, a, 2 * P * (m % 2) : 2 * P * (m % 2 + 1)]
                 for lo in range(0, cols, step):
                     nc.tensor.matmul_mx(
                         out=banks[c, m][:, lo : lo + step],
@@ -113,16 +112,17 @@ def tile_list_hscat_silu_kernel(tc, x, w_words, w_scales, b, wgo, offs, out):
 
         with nc.allow_non_contiguous_dma(reason="512 bias values, one to a partition and block"):
             nc.scalar.dma_start(b_sb[:], b.rearrange("(m p) -> p m", p=P))
-        nc.vector.memset(tiny[:], 0.0)
+        nc.gpsimd.memset(tiny[:], 0.0)
         nc.scalar.activation(tiny[:, 0:1], tiny[:, 1:2], SILU)
         load(0, 0)
         for q in range(4):
             nc.sync.dma_start(ws_sb[32 * q : 32 * q + 4, :, :].bitcast(I32), w_scales[:, 4 * q : 4 * q + 4, :].rearrange("a q n -> q a n").bitcast(I32))
         for a in range(1, PASSES):
             load(0, a)
-        nc.sync.dma_start(w_sb[:].bitcast(I32), w_view.bitcast(I32))
+        nc.sync.dma_start(w_sb[0][:].bitcast(I32), w_view[:, :, 0:M].bitcast(I32))
         nc.sync.dma_start(offs_sb[:], offs)
         load_wgo(0, 256)
+        nc.sync.dma_start(w_sb[1][:].bitcast(I32), w_view[:, :, M : 2 * M].bitcast(I32))
         for c in range(1, LAST + 1):
             for a in range(PASSES):
                 load(c, a)
@@ -133,18 +133,12 @@ def tile_list_hscat_silu_kernel(tc, x, w_words, w_scales, b, wgo, offs, out):
         clear(nc.vector, 0, [0, 2047, T])
         clear(nc.gpsimd, 1, [0, T])
         clear(nc.gpsimd, 2, list(range(0, T + 1, 512)))
-        clear(nc.gpsimd, 3, list(range(T // 2, T + 1, 512)))
+        clear(nc.gpsimd, 3, list(range(T // 2, T + 1, 256)))
 
-        def lag(c, m):
-            if c == 0:
-                return m if m < BLOCKS - 1 else PASSES
-            return m + 1 if m < (BLOCKS - 1 if c < LAST - 1 else 2) else PASSES + (m == BLOCKS - 1 and c == LAST - 1)
-
-        held = {}
-        for c in range(LAST):
-            for m in range(BLOCKS):
-                held[PASSES * c + PASSES - 1 + lag(c, m)] = (c, m)
-        y_tail = raw[LAST, PASSES - 1][:, 2:4, :].rearrange("p i j -> p (i j)")
+        held = {PASSES * (c + 1) + m: (c, m) for c in range(1, LAST - 1) for m in range(BLOCKS)}
+        held.update({PASSES: (0, 1), PASSES + 1: (0, 2), 2 * PASSES - 1: (0, 3)})
+        tails = [raw[LAST, m][:, 0:2, :].rearrange("p i j -> p (i j)") for m in range(BLOCKS)]
+        early = [WIDTHS[LAST - 1] if m == 0 else 256 for m in range(BLOCKS)]
 
         for step in range(PASSES * (LAST + 1)):
             c, a = divmod(step, PASSES)
@@ -156,16 +150,13 @@ def tile_list_hscat_silu_kernel(tc, x, w_words, w_scales, b, wgo, offs, out):
                     multiply(c, m)
             if step == PASSES - 1:
                 place_now(0, 0)
+            elif c == LAST:
+                activate(c - 1, a, tails[a][:, 0 : WIDTHS[c - 1]])
+                scatter(a, STARTS[c - 1], STARTS[c - 1] + early[a], tails[a][:, 0 : early[a]])
             elif step in held:
                 hc, hm = held[step]
-                if (c, a) == (LAST - 1, 1):
-                    place(hc, hm, raw[c, 0][:, 1, 0 : WIDTHS[hc]])
-                else:
-                    place(hc, hm, raw[c, a][:, 0, 0 : WIDTHS[hc]])
-        activate(LAST - 1, BLOCKS - 1, y_tail[:, 0 : WIDTHS[LAST - 1]])
-        for m in range(BLOCKS - 1):
-            place_now(LAST, m)
+                place(hc, hm, raw[c, a][:, 0, 0 : WIDTHS[hc]])
+        for m in range(BLOCKS):
+            activate(LAST, m, tails[m][:, WIDTHS[LAST - 1] :])
+            scatter(m, STARTS[LAST - 1] + early[m], S, tails[m][:, early[m] :])
             store(m)
-        activate(LAST, BLOCKS - 1, y_tail[:, WIDTHS[LAST - 1] :])
-        scatter(BLOCKS - 1, STARTS[LAST - 1], S, y_tail)
-        store(BLOCKS - 1)

@@ -30,8 +30,8 @@ def tile_list_hscat_silu_kernel(tc, x, w_words, w_scales, b, wgo, offs, out):
     with ExitStack() as ctx:
         keep = ctx.enter_context(tc.tile_pool(name="keep", bufs=1))
         stage = ctx.enter_context(tc.tile_pool(name="stage", bufs=1))
-        group = ctx.enter_context(tc.tile_pool(name="group", bufs=5))
-        quant = ctx.enter_context(tc.tile_pool(name="quant", bufs=6))
+        group = ctx.enter_context(tc.tile_pool(name="group", bufs=3))
+        quant = ctx.enter_context(tc.tile_pool(name="quant", bufs=4))
         result = ctx.enter_context(tc.tile_pool(name="result", bufs=1))
         psum = ctx.enter_context(tc.psum_pool(name="psum", bufs=1))
 
@@ -65,16 +65,19 @@ def tile_list_hscat_silu_kernel(tc, x, w_words, w_scales, b, wgo, offs, out):
         def interleave(dst, src, engine):
             engine(dst.rearrange("p (c i) t -> p c t i", i=4), src.rearrange("p t (c i) -> p c t i", i=4))
 
-        def quantize(c, a):
+        def quantize(c, passes):
             cols = WIDTHS[c]
-            grouped = group.tile([P, cols, 4], BF16, name="grouped", align_bytes=64)
-            codes[c, a] = quant.tile([P, cols], U32, name="codes", align_bytes=64)
-            scales[c, a] = quant.tile([P, cols], U8, name="scales", align_bytes=64)
-            split = 96 if (c, a) == (0, PASSES - 1) else cols
-            interleave(grouped[:, 0:split, :], raw[c, a][:, :, 0:split], nc.scalar.copy)
-            if split < cols:
-                interleave(grouped[:, split:cols, :], raw[c, a][:, :, split:cols], nc.vector.tensor_copy)
-            nc.vector.quantize_mx(out=codes[c, a][:].bitcast(E4M3), scales=scales[c, a][:], in_=grouped[:].rearrange("p c t -> p (c t)"))
+            grouped = group.tile([P, len(passes), cols, 4], BF16, name="grouped", align_bytes=64)
+            words = quant.tile([P, len(passes) * cols], U32, name="words", align_bytes=64)
+            plane = quant.tile([P, len(passes) * cols], U8, name="plane", align_bytes=64)
+            for i, a in enumerate(passes):
+                split = 96 if (c, a) == (0, PASSES - 1) else cols
+                interleave(grouped[:, i, 0:split, :], raw[c, a][:, :, 0:split], nc.scalar.copy)
+                if split < cols:
+                    interleave(grouped[:, i, split:cols, :], raw[c, a][:, :, split:cols], nc.vector.tensor_copy)
+                codes[c, a] = words[:, i * cols : (i + 1) * cols]
+                scales[c, a] = plane[:, i * cols : (i + 1) * cols]
+            nc.vector.quantize_mx(out=words[:].bitcast(E4M3), scales=plane[:], in_=grouped[:].rearrange("p a c t -> p (a c t)"))
 
         def multiply(c, m):
             cols = WIDTHS[c]
@@ -126,36 +129,45 @@ def tile_list_hscat_silu_kernel(tc, x, w_words, w_scales, b, wgo, offs, out):
         for c in range(1, LAST + 1):
             for a in range(PASSES):
                 load(c, a)
-            if c == 1:
-                load_wgo(256, 1024)
-            if c >= LAST - 1:
-                load_wgo(STARTS[c], STARTS[c] + WIDTHS[c])
+                if (c, a) == (2, 1):
+                    load_wgo(STARTS[1], STARTS[LAST - 1])
+                if (c, a) == (LAST, 1):
+                    load_wgo(STARTS[LAST - 1], STARTS[LAST])
+        load_wgo(STARTS[LAST], S)
         clear(nc.vector, 0, [0, 2047, T])
         clear(nc.gpsimd, 1, [0, T])
         clear(nc.gpsimd, 2, list(range(0, T + 1, 512)))
         clear(nc.gpsimd, 3, list(range(T // 2, T + 1, 256)))
 
-        held = {PASSES * (c + 1) + m: (c, m) for c in range(1, LAST - 1) for m in range(BLOCKS)}
-        held.update({PASSES: (0, 1), PASSES + 1: (0, 2), 2 * PASSES - 1: (0, 3)})
-        tails = [raw[LAST, m][:, 0:2, :].rearrange("p i j -> p (i j)") for m in range(BLOCKS)]
+        tails = [raw[LAST, 1 + m // 2 * 2][:, m % 2 * 2 : m % 2 * 2 + 2, :].rearrange("p i j -> p (i j)") for m in range(BLOCKS)]
         early = [WIDTHS[LAST - 1] if m == 0 else 256 for m in range(BLOCKS)]
 
-        for step in range(PASSES * (LAST + 1)):
-            c, a = divmod(step, PASSES)
-            quantize(c, a)
+        def multiply_all(c):
+            for m in range(BLOCKS):
+                multiply(c, m)
+
+        for a in range(PASSES):
+            quantize(0, [a])
+        clear(nc.vector, 3, [0, 511, 1024, 1535, T // 2])
+        multiply_all(0)
+        place_now(0, 0)
+        for a, m in ((0, 1), (1, 2), (2, None), (3, 3)):
+            quantize(1, [a])
             if a == PASSES - 1:
-                if c == 0:
-                    clear(nc.vector, 3, [0, 511, 1024, 1535, T // 2])
-                for m in range(BLOCKS):
-                    multiply(c, m)
-            if step == PASSES - 1:
-                place_now(0, 0)
-            elif c == LAST:
-                activate(c - 1, a, tails[a][:, 0 : WIDTHS[c - 1]])
-                scatter(a, STARTS[c - 1], STARTS[c - 1] + early[a], tails[a][:, 0 : early[a]])
-            elif step in held:
-                hc, hm = held[step]
-                place(hc, hm, raw[c, a][:, 0, 0 : WIDTHS[hc]])
+                multiply_all(1)
+            if m is not None:
+                place(0, m, raw[1, a][:, 0, :])
+        for c in range(2, LAST + 1):
+            for pair in ([0, 1], [2, 3]):
+                quantize(c, pair)
+                if pair[1] == PASSES - 1:
+                    multiply_all(c)
+                for m in pair:
+                    if c < LAST:
+                        place(c - 1, m, raw[c, pair[1]][:, m % 2, 0 : WIDTHS[c - 1]])
+                    else:
+                        activate(c - 1, m, tails[m][:, 0 : WIDTHS[c - 1]])
+                        scatter(m, STARTS[c - 1], STARTS[c - 1] + early[m], tails[m][:, 0 : early[m]])
         for m in range(BLOCKS):
             activate(LAST, m, tails[m][:, WIDTHS[LAST - 1] :])
             scatter(m, STARTS[LAST - 1] + early[m], S, tails[m][:, early[m] :])

@@ -20,19 +20,18 @@ BLOCKS = M // P
 BANK = 512
 FLOPS = 2 * K * M * S
 
-WIDTHS = [256, 256, 256, 256, 512, 512]
-STARTS = [sum(WIDTHS[:c]) for c in range(len(WIDTHS))]
-LAST = len(WIDTHS) - 1
+WIDTH = 256
+CHUNKS = S // WIDTH
+LAST = CHUNKS - 1
+KEPT = 704
 
 
 def tile_list_hscat_silu_kernel(tc, x, w_words, w_scales, b, wgo, offs, out):
     nc = tc.nc
     with ExitStack() as ctx:
         keep = ctx.enter_context(tc.tile_pool(name="keep", bufs=1))
-        stage = ctx.enter_context(tc.tile_pool(name="stage", bufs=1))
-        group = ctx.enter_context(tc.tile_pool(name="group", bufs=3))
+        group = ctx.enter_context(tc.tile_pool(name="group", bufs=4))
         quant = ctx.enter_context(tc.tile_pool(name="quant", bufs=4))
-        result = ctx.enter_context(tc.tile_pool(name="result", bufs=1))
         psum = ctx.enter_context(tc.psum_pool(name="psum", bufs=1))
 
         offs_sb = keep.tile([P, S // 16], U16, name="offs_sb")
@@ -41,77 +40,88 @@ def tile_list_hscat_silu_kernel(tc, x, w_words, w_scales, b, wgo, offs, out):
         b_sb = keep.tile([P, BLOCKS], F32, name="b_sb")
         tiny = keep.tile([P, 8], F32, name="tiny")
         wgo_sb = keep.tile([P, S], F32, name="wgo_sb")
-        windows = [keep.tile([P, T], F32, name=f"window{m}") for m in range(BLOCKS)]
+        first = keep.tile([P, 2 * WIDTH], F32, name="first")
+        windows = [keep.tile([P, T], F32, name=f"window{m}") for m in range(BLOCKS - 1)]
+        raw = {(c, a): keep.tile([P, 4, WIDTH], F32, name=f"raw{c}{a}") for c in range(CHUNKS) for a in range(PASSES)}
+        banks = {(m, h): psum.tile([P, BANK], F32, name=f"bank{m}{h}") for m in range(BLOCKS) for h in range(2)}
         w_view = w_words.rearrange("a p c -> p a c")
 
-        raw = {}
-        banks = {}
+        grouped = {}
         codes = {}
         scales = {}
 
         def load(c, a):
-            cols = WIDTHS[c]
-            t = stage.tile([P, 4, cols], F32, name="raw", tag=f"raw{cols}", bufs=12 if cols == 256 else 8)
-            nc.sync.dma_start(t[:], x[512 * a : 512 * a + 512, STARTS[c] : STARTS[c] + cols].rearrange("(p i) j -> p i j", i=4))
-            raw[c, a] = t
+            nc.sync.dma_start(raw[c, a][:], x[512 * a : 512 * a + 512, WIDTH * c : WIDTH * (c + 1)].rearrange("(p i) j -> p i j", i=4))
 
         def load_wgo(lo, hi):
-            nc.sync.dma_start(wgo_sb[:, lo:hi], wgo[:, lo:hi])
+            nc.sync.dma_start(wgo_sb[:, WIDTH * lo : WIDTH * hi], wgo[:, WIDTH * lo : WIDTH * hi])
 
         def clear(engine, m, cuts):
             for lo, hi in zip(cuts[:-1], cuts[1:]):
                 engine.memset(windows[m][:, lo:hi], 0.0)
 
-        def interleave(dst, src, engine):
+        def weave(dst, src, engine):
             engine(dst.rearrange("p (c i) t -> p c t i", i=4), src.rearrange("p t (c i) -> p c t i", i=4))
 
-        def quantize(c, passes):
-            cols = WIDTHS[c]
-            grouped = group.tile([P, len(passes), cols, 4], BF16, name="grouped", align_bytes=64)
-            words = quant.tile([P, len(passes) * cols], U32, name="words", align_bytes=64)
-            plane = quant.tile([P, len(passes) * cols], U8, name="plane", align_bytes=64)
+        def interleave(c, passes):
+            if (c, passes[-1]) == (0, PASSES - 1):
+                t = keep.tile([P, 1, WIDTH, 4], BF16, name="grouped_first", tag="late", align_bytes=64)
+            else:
+                t = group.tile([P, len(passes), WIDTH, 4], BF16, name="grouped", align_bytes=64)
             for i, a in enumerate(passes):
-                split = 96 if (c, a) == (0, PASSES - 1) else cols
-                interleave(grouped[:, i, 0:split, :], raw[c, a][:, :, 0:split], nc.scalar.copy)
-                if split < cols:
-                    interleave(grouped[:, i, split:cols, :], raw[c, a][:, :, split:cols], nc.vector.tensor_copy)
-                codes[c, a] = words[:, i * cols : (i + 1) * cols]
-                scales[c, a] = plane[:, i * cols : (i + 1) * cols]
-            nc.vector.quantize_mx(out=words[:].bitcast(E4M3), scales=plane[:], in_=grouped[:].rearrange("p a c t -> p (a c t)"))
+                split = 96 if (c, a) in ((0, 3),) else WIDTH
+                weave(t[:, i, 0:split, :], raw[c, a][:, :, 0:split], nc.scalar.copy)
+                if split < WIDTH:
+                    weave(t[:, i, split:WIDTH, :], raw[c, a][:, :, split:WIDTH], nc.vector.tensor_copy)
+            grouped[c, passes[0]] = t
 
-        def multiply(c, m):
-            cols = WIDTHS[c]
-            step = BANK if cols == BANK else P
-            banks[c, m] = psum.tile([P, BANK], F32, name=f"bank{c % 2}{m}")
-            for a in range(PASSES):
-                words = w_sb[m // 2][:, a, 2 * P * (m % 2) : 2 * P * (m % 2 + 1)]
-                for lo in range(0, cols, step):
-                    nc.tensor.matmul_mx(
-                        out=banks[c, m][:, lo : lo + step],
-                        lhsT=words.bitcast(E2M1),
-                        lhsT_scale=ws_sb[:, a, P * m : P * (m + 1)],
-                        rhs=codes[c, a][:, lo : lo + step].bitcast(E4M3),
-                        rhs_scale=scales[c, a][:, lo : lo + step],
-                        start=(a == 0 and lo == 0),
-                        stop=(a == PASSES - 1 and lo + step == cols),
-                    )
+        def quantize(c, passes):
+            words = quant.tile([P, len(passes) * WIDTH], U32, name="words", align_bytes=64)
+            plane = quant.tile([P, len(passes) * WIDTH], U8, name="plane", align_bytes=64)
+            for i, a in enumerate(passes):
+                codes[c, a] = words[:, i * WIDTH : (i + 1) * WIDTH]
+                scales[c, a] = plane[:, i * WIDTH : (i + 1) * WIDTH]
+            nc.vector.quantize_mx(out=words[:].bitcast(E4M3), scales=plane[:], in_=grouped[c, passes[0]][:].rearrange("p a c t -> p (a c t)"))
 
-        def activate(c, m, y):
-            nc.scalar.activation(y, banks[c, m][:, 0 : WIDTHS[c]], SILU, bias=b_sb[:, m : m + 1])
+        def sums(m, lo, hi):
+            c = lo // WIDTH
+            if m == 0:
+                return banks[m, c % 2][:, 0 : hi - lo]
+            return banks[m, c // 2 % 2 if c else 1][:, lo % BANK : lo % BANK + hi - lo]
+
+        def multiply(c, passes, blocks):
+            for m in blocks:
+                for a in passes:
+                    words = w_sb[m // 2][:, a, 2 * P * (m % 2) : 2 * P * (m % 2 + 1)]
+                    for lo in range(0, WIDTH, P):
+                        nc.tensor.matmul_mx(
+                            out=sums(m, WIDTH * c, WIDTH * (c + 1))[:, lo : lo + P],
+                            lhsT=words.bitcast(E2M1),
+                            lhsT_scale=ws_sb[:, a, P * m : P * (m + 1)],
+                            rhs=codes[c, a][:, lo : lo + P].bitcast(E4M3),
+                            rhs_scale=scales[c, a][:, lo : lo + P],
+                            start=(a == 0 and lo == 0),
+                            stop=(a == PASSES - 1 and lo + P == WIDTH),
+                        )
+
+        def activate(m, lo, hi, y):
+            nc.scalar.activation(y, sums(m, lo, hi), SILU, bias=b_sb[:, m : m + 1])
 
         def scatter(m, lo, hi, y):
             nc.vector.tensor_tensor(windows[m][:].indirect(offs_sb[:, lo // 16 : hi // 16]), y, wgo_sb[:, lo:hi], MULT)
 
-        def place(c, m, y):
-            activate(c, m, y)
-            scatter(m, STARTS[c], STARTS[c] + WIDTHS[c], y)
+        def flat(c, a):
+            return raw[c, a][:].rearrange("p i j -> p (i j)")
 
-        def place_now(c, m):
-            y = result.tile([P, WIDTHS[c]], F32, name="y")
-            place(c, m, y[:])
-
-        def store(m):
-            nc.sync.dma_start(out[P * m : P * (m + 1), :], windows[m][:])
+        def step(c, passes, placed, urgent=()):
+            interleave(c, passes)
+            homes = [flat(c, passes[0])[:, BANK * i : BANK * i + hi - lo] for i, (m, lo, hi) in enumerate(placed)]
+            for (m, lo, hi), y in zip(placed, homes):
+                activate(m, lo, hi, y)
+            quantize(c, passes)
+            multiply(c, passes, list(urgent) + [m for m in range(BLOCKS) if m not in urgent])
+            for (m, lo, hi), y in zip(placed, homes):
+                scatter(m, lo, hi, y)
 
         with nc.allow_non_contiguous_dma(reason="512 bias values, one to a partition and block"):
             nc.scalar.dma_start(b_sb[:], b.rearrange("(m p) -> p m", p=P))
@@ -124,51 +134,49 @@ def tile_list_hscat_silu_kernel(tc, x, w_words, w_scales, b, wgo, offs, out):
             load(0, a)
         nc.sync.dma_start(w_sb[0][:].bitcast(I32), w_view[:, :, 0:M].bitcast(I32))
         nc.sync.dma_start(offs_sb[:], offs)
-        load_wgo(0, 256)
+        load_wgo(0, 1)
         nc.sync.dma_start(w_sb[1][:].bitcast(I32), w_view[:, :, M : 2 * M].bitcast(I32))
-        for c in range(1, LAST + 1):
+        for c in range(1, CHUNKS):
             for a in range(PASSES):
                 load(c, a)
-                if (c, a) == (2, 1):
-                    load_wgo(STARTS[1], STARTS[LAST - 1])
-                if (c, a) == (LAST, 1):
-                    load_wgo(STARTS[LAST - 1], STARTS[LAST])
-        load_wgo(STARTS[LAST], S)
+                if a == 1 and c % 2 == 0:
+                    load_wgo(c - 1, c + 1)
+        load_wgo(LAST, CHUNKS)
         clear(nc.vector, 0, [0, 2047, T])
         clear(nc.gpsimd, 1, [0, T])
-        clear(nc.gpsimd, 2, list(range(0, T + 1, 512)))
-        clear(nc.gpsimd, 3, list(range(T // 2, T + 1, 256)))
+        clear(nc.vector, 2, [0, 1023, T // 2])
+        clear(nc.gpsimd, 2, [T // 2, T])
 
-        tails = [raw[LAST, 1 + m // 2 * 2][:, m % 2 * 2 : m % 2 * 2 + 2, :].rearrange("p i j -> p (i j)") for m in range(BLOCKS)]
-        early = [WIDTHS[LAST - 1] if m == 0 else 256 for m in range(BLOCKS)]
+        for passes in ([0, 1], [2], [3]):
+            interleave(0, passes)
+            quantize(0, passes)
+        windows.append(keep.tile([P, T], F32, name="window3", tag="late", align_bytes=64))
+        clear(nc.gpsimd, 3, list(range(0, T + 1, 256)))
+        multiply(0, range(PASSES), range(BLOCKS))
+        for m in range(2):
+            y = first[:, WIDTH * m : WIDTH * (m + 1)]
+            activate(m, 0, WIDTH, y)
+            scatter(m, 0, WIDTH, y)
+        step(1, [0, 1], [(2, 0, WIDTH)])
+        step(1, [2, 3], [(3, 0, WIDTH)], [1, 2])
+        cuts = [WIDTH, 2 * WIDTH, 3 * WIDTH, 4 * WIDTH, S - KEPT]
+        waiting = [(m, lo, hi) for lo, hi in zip(cuts[:-1], cuts[1:]) for m in range(1, BLOCKS)]
+        for c in range(2, CHUNKS):
+            newest = (0, WIDTH * (c - 1), WIDTH * c)
+            older = waiting[2 * (c - 2) : 2 * (c - 1)]
+            if c < LAST:
+                step(c, [0, 1], older)
+                step(c, [2, 3], [newest], [m for m, lo, hi in waiting[2 * (c - 1) : 2 * c]] if c + 1 < LAST else [0])
+            else:
+                step(c, [0, 1], [older[0], newest])
+                step(c, [2, 3], [older[1]])
 
-        def multiply_all(c):
-            for m in range(BLOCKS):
-                multiply(c, m)
-
-        for a in range(PASSES):
-            quantize(0, [a])
-        clear(nc.vector, 3, [0, 511, 1024, 1535, T // 2])
-        multiply_all(0)
-        place_now(0, 0)
-        for a, m in ((0, 1), (1, 2), (2, None), (3, 3)):
-            quantize(1, [a])
-            if a == PASSES - 1:
-                multiply_all(1)
-            if m is not None:
-                place(0, m, raw[1, a][:, 0, :])
-        for c in range(2, LAST + 1):
-            for pair in ([0, 1], [2, 3]):
-                quantize(c, pair)
-                if pair[1] == PASSES - 1:
-                    multiply_all(c)
-                for m in pair:
-                    if c < LAST:
-                        place(c - 1, m, raw[c, pair[1]][:, m % 2, 0 : WIDTHS[c - 1]])
-                    else:
-                        activate(c - 1, m, tails[m][:, 0 : WIDTHS[c - 1]])
-                        scatter(m, STARTS[c - 1], STARTS[c - 1] + early[m], tails[m][:, 0 : early[m]])
-        for m in range(BLOCKS):
-            activate(LAST, m, tails[m][:, WIDTHS[LAST - 1] :])
-            scatter(m, STARTS[LAST - 1] + early[m], S, tails[m][:, early[m] :])
-            store(m)
+        y = flat(LAST, PASSES - 1)[:, 0:WIDTH]
+        activate(0, S - WIDTH, S, y)
+        scatter(0, S - WIDTH, S, y)
+        nc.sync.dma_start(out[0:P, :], windows[0][:])
+        for m, home in ((1, flat(LAST, 1)), (2, flat(LAST - 1, 1)), (3, flat(LAST - 1, 3))):
+            activate(m, S - KEPT, S - BANK, home[:, 0 : KEPT - BANK])
+            activate(m, S - BANK, S, home[:, KEPT - BANK : KEPT])
+            scatter(m, S - KEPT, S, home[:, 0:KEPT])
+            nc.sync.dma_start(out[P * m : P * (m + 1), :], windows[m][:])

@@ -21,8 +21,10 @@ BANK = 512
 FLOPS = 2 * K * M * S
 
 WIDTH = 256
-CHUNKS = S // WIDTH
-LAST = CHUNKS - 1
+NARROW = 4
+MID = NARROW * WIDTH
+END = MID + BANK
+LEAD = 32
 KEPT = 704
 
 
@@ -35,26 +37,30 @@ def tile_list_hscat_silu_kernel(tc, x, w_words, w_scales, b, wgo, offs, out):
         psum = ctx.enter_context(tc.psum_pool(name="psum", bufs=1))
 
         offs_sb = keep.tile([P, S // 16], U16, name="offs_sb")
-        w_sb = [keep.tile([P, PASSES, M], U8, name=f"w_sb{h}", align_bytes=64) for h in range(2)]
+        w_sb = keep.tile([P, PASSES, 2 * M], U8, name="w_sb", align_bytes=64)
         ws_sb = keep.tile([P, PASSES, M], U8, name="ws_sb", align_bytes=64)
         b_sb = keep.tile([P, BLOCKS], F32, name="b_sb")
         tiny = keep.tile([P, 8], F32, name="tiny")
         wgo_sb = keep.tile([P, S], F32, name="wgo_sb")
-        first = keep.tile([P, 2 * WIDTH], F32, name="first")
+        first = keep.tile([P, 3 * WIDTH], F32, name="first")
         windows = [keep.tile([P, T], F32, name=f"window{m}") for m in range(BLOCKS - 1)]
-        raw = {(c, a): keep.tile([P, 4, WIDTH], F32, name=f"raw{c}{a}") for c in range(CHUNKS) for a in range(PASSES)}
+        x_sb = keep.tile([P, K * S // P], F32, name="x_sb")
+        raw = {}
+        start = {}
         banks = {(m, h): psum.tile([P, BANK], F32, name=f"bank{m}{h}") for m in range(BLOCKS) for h in range(2)}
         w_view = w_words.rearrange("a p c -> p a c")
 
-        grouped = {}
         codes = {}
         scales = {}
 
-        def load(c, a):
-            nc.sync.dma_start(raw[c, a][:], x[512 * a : 512 * a + 512, WIDTH * c : WIDTH * (c + 1)].rearrange("(p i) j -> p i j", i=4))
+        def load(lo, hi, a):
+            at = sum(4 * t.shape[2] for t in raw.values())
+            start[lo, a] = at
+            raw[lo, a] = x_sb[:, at : at + 4 * (hi - lo)].rearrange("p (i j) -> p i j", i=4)
+            nc.sync.dma_start(raw[lo, a], x[512 * a : 512 * a + 512, lo:hi].rearrange("(p i) j -> p i j", i=4))
 
         def load_wgo(lo, hi):
-            nc.sync.dma_start(wgo_sb[:, WIDTH * lo : WIDTH * hi], wgo[:, WIDTH * lo : WIDTH * hi])
+            nc.sync.dma_start(wgo_sb[:, lo:hi], wgo[:, lo:hi])
 
         def clear(engine, m, cuts):
             for lo, hi in zip(cuts[:-1], cuts[1:]):
@@ -63,45 +69,52 @@ def tile_list_hscat_silu_kernel(tc, x, w_words, w_scales, b, wgo, offs, out):
         def weave(dst, src, engine):
             engine(dst.rearrange("p (c i) t -> p c t i", i=4), src.rearrange("p t (c i) -> p c t i", i=4))
 
-        def interleave(c, passes):
-            if (c, passes[-1]) == (0, PASSES - 1):
-                t = keep.tile([P, 1, WIDTH, 4], BF16, name="grouped_first", tag="late", align_bytes=64)
+        def interleave(lo, hi, passes, lead=0):
+            cols = hi - lo
+            if (lo, passes[-1]) == (0, PASSES - 1):
+                t = keep.tile([P, 1, cols, 4], BF16, name="grouped_first", tag="late", align_bytes=64)
             else:
-                t = group.tile([P, len(passes), WIDTH, 4], BF16, name="grouped", align_bytes=64)
+                t = group.tile([P, len(passes), cols, 4], BF16, name="grouped", align_bytes=64)
             for i, a in enumerate(passes):
-                split = 96 if (c, a) in ((0, 3),) else WIDTH
-                weave(t[:, i, 0:split, :], raw[c, a][:, :, 0:split], nc.scalar.copy)
-                if split < WIDTH:
-                    weave(t[:, i, split:WIDTH, :], raw[c, a][:, :, split:WIDTH], nc.vector.tensor_copy)
-            grouped[c, passes[0]] = t
+                split = 96 if a == PASSES - 1 and lo < 1 * WIDTH else cols
+                cuts = [0, lead, split] if lead and a == passes[-1] else [0, split]
+                for c0, c1 in zip(cuts[:-1], cuts[1:]):
+                    weave(t[:, i, c0:c1, :], raw[lo, a][:, :, c0:c1], nc.scalar.copy)
+                if split < cols:
+                    weave(t[:, i, split:cols, :], raw[lo, a][:, :, split:cols], nc.vector.tensor_copy)
+            return t
 
-        def quantize(c, passes):
-            words = quant.tile([P, len(passes) * WIDTH], U32, name="words", align_bytes=64)
-            plane = quant.tile([P, len(passes) * WIDTH], U8, name="plane", align_bytes=64)
+        def quantize(grouped, lo, hi, passes):
+            cols = hi - lo
+            words = quant.tile([P, len(passes) * cols], U32, name="words", align_bytes=64)
+            plane = quant.tile([P, len(passes) * cols], U8, name="plane", align_bytes=64)
             for i, a in enumerate(passes):
-                codes[c, a] = words[:, i * WIDTH : (i + 1) * WIDTH]
-                scales[c, a] = plane[:, i * WIDTH : (i + 1) * WIDTH]
-            nc.vector.quantize_mx(out=words[:].bitcast(E4M3), scales=plane[:], in_=grouped[c, passes[0]][:].rearrange("p a c t -> p (a c t)"))
+                codes[a] = words[:, i * cols : (i + 1) * cols]
+                scales[a] = plane[:, i * cols : (i + 1) * cols]
+            nc.vector.quantize_mx(out=words[:].bitcast(E4M3), scales=plane[:], in_=grouped[:].rearrange("p a c t -> p (a c t)"))
 
         def sums(m, lo, hi):
-            c = lo // WIDTH
             if m == 0:
-                return banks[m, c % 2][:, 0 : hi - lo]
-            return banks[m, c // 2 % 2 if c else 1][:, lo % BANK : lo % BANK + hi - lo]
+                starts = [WIDTH * c for c in range(NARROW)] + [MID, END]
+                c = max(i for i, at in enumerate(starts) if at <= lo)
+                return banks[m, c % 2][:, lo - starts[c] : hi - starts[c]]
+            return banks[m, lo // BANK % 2 if lo >= WIDTH else 1][:, lo % BANK : lo % BANK + hi - lo]
 
-        def multiply(c, passes, blocks):
+        def multiply(lo, hi, passes, blocks):
             for m in blocks:
+                size = hi - lo
+                n = BANK if size == hi - lo == BANK else P
                 for a in passes:
-                    words = w_sb[m // 2][:, a, 2 * P * (m % 2) : 2 * P * (m % 2 + 1)]
-                    for lo in range(0, WIDTH, P):
+                    words = w_sb[:, a, 2 * P * m : 2 * P * (m + 1)]
+                    for at in range(lo, hi, n):
                         nc.tensor.matmul_mx(
-                            out=sums(m, WIDTH * c, WIDTH * (c + 1))[:, lo : lo + P],
+                            out=sums(m, at, at + n),
                             lhsT=words.bitcast(E2M1),
                             lhsT_scale=ws_sb[:, a, P * m : P * (m + 1)],
-                            rhs=codes[c, a][:, lo : lo + P].bitcast(E4M3),
-                            rhs_scale=scales[c, a][:, lo : lo + P],
-                            start=(a == 0 and lo == 0),
-                            stop=(a == PASSES - 1 and lo + P == WIDTH),
+                            rhs=codes[a][:, at - lo : at - lo + n].bitcast(E4M3),
+                            rhs_scale=scales[a][:, at - lo : at - lo + n],
+                            start=(a == 0 and at % size == 0),
+                            stop=(a == PASSES - 1 and (at + n) % size == 0),
                         )
 
         def activate(m, lo, hi, y):
@@ -110,73 +123,83 @@ def tile_list_hscat_silu_kernel(tc, x, w_words, w_scales, b, wgo, offs, out):
         def scatter(m, lo, hi, y):
             nc.vector.tensor_tensor(windows[m][:].indirect(offs_sb[:, lo // 16 : hi // 16]), y, wgo_sb[:, lo:hi], MULT)
 
-        def flat(c, a):
-            return raw[c, a][:].rearrange("p i j -> p (i j)")
+        def flat(lo, a):
+            return x_sb[:, start[lo, a] : start[lo, a] + 2 * BANK]
 
-        def step(c, passes, placed, urgent=()):
-            interleave(c, passes)
-            homes = [flat(c, passes[0])[:, BANK * i : BANK * i + hi - lo] for i, (m, lo, hi) in enumerate(placed)]
-            for (m, lo, hi), y in zip(placed, homes):
-                activate(m, lo, hi, y)
-            quantize(c, passes)
-            multiply(c, passes, list(urgent) + [m for m in range(BLOCKS) if m not in urgent])
-            for (m, lo, hi), y in zip(placed, homes):
-                scatter(m, lo, hi, y)
+        def step(lo, hi, passes, placed, urgent=0):
+            grouped = interleave(lo, hi, passes, LEAD if placed else 0)
+            end = start[lo, passes[-1]] + LEAD
+            ys = [x_sb[:, end - BANK * i - (to - at) : end - BANK * i] for i, (m, at, to) in enumerate(placed)]
+            for piece, y in zip(placed, ys):
+                activate(*piece, y)
+            quantize(grouped, lo, hi, passes)
+            if passes[-1] == PASSES - 1:
+                multiply(lo, hi, range(PASSES), [(urgent + i) % BLOCKS for i in range(BLOCKS)])
+            for piece, y in zip(placed, ys):
+                scatter(*piece, y)
 
-        with nc.allow_non_contiguous_dma(reason="512 bias values, one to a partition and block"):
-            nc.scalar.dma_start(b_sb[:], b.rearrange("(m p) -> p m", p=P))
         nc.gpsimd.memset(tiny[:], 0.0)
         nc.scalar.activation(tiny[:, 0:1], tiny[:, 1:2], SILU)
-        load(0, 0)
+        load(0, WIDTH, 0)
+        load(0, WIDTH, 1)
+        load(0, WIDTH, 2)
+        load(0, WIDTH, 3)
         for q in range(4):
             nc.sync.dma_start(ws_sb[32 * q : 32 * q + 4, :, :].bitcast(I32), w_scales[:, 4 * q : 4 * q + 4, :].rearrange("a q n -> q a n").bitcast(I32))
-        for a in range(1, PASSES):
-            load(0, a)
-        nc.sync.dma_start(w_sb[0][:].bitcast(I32), w_view[:, :, 0:M].bitcast(I32))
+        nc.sync.dma_start(w_sb[:].bitcast(I32), w_view.bitcast(I32))
+        with nc.allow_non_contiguous_dma(reason="512 bias values, one to a partition and block"):
+            nc.sync.dma_start(b_sb[:], b.rearrange("(m p) -> p m", p=P))
         nc.sync.dma_start(offs_sb[:], offs)
-        load_wgo(0, 1)
-        nc.sync.dma_start(w_sb[1][:].bitcast(I32), w_view[:, :, M : 2 * M].bitcast(I32))
-        for c in range(1, CHUNKS):
+        load_wgo(0, WIDTH)
+        for lo in range(WIDTH, MID, WIDTH):
             for a in range(PASSES):
-                load(c, a)
-                if a == 1 and c % 2 == 0:
-                    load_wgo(c - 1, c + 1)
-        load_wgo(LAST, CHUNKS)
+                load(lo, lo + WIDTH, a)
+                if (lo, a) == (2 * WIDTH, 0):
+                    load_wgo(WIDTH, 3 * WIDTH)
+        for lo in (MID, END):
+            for a in range(PASSES):
+                load(lo, lo + BANK, a)
+                if a == 0:
+                    load_wgo(lo - (WIDTH if lo == MID else BANK), lo)
+        load_wgo(END, S)
         clear(nc.vector, 0, [0, 2047, T])
         clear(nc.gpsimd, 1, [0, T])
         clear(nc.vector, 2, [0, 1023, T // 2])
         clear(nc.gpsimd, 2, [T // 2, T])
 
         for passes in ([0, 1], [2], [3]):
-            interleave(0, passes)
-            quantize(0, passes)
+            quantize(interleave(0, WIDTH, passes), 0, WIDTH, passes)
         windows.append(keep.tile([P, T], F32, name="window3", tag="late", align_bytes=64))
         clear(nc.gpsimd, 3, list(range(0, T + 1, 256)))
-        multiply(0, range(PASSES), range(BLOCKS))
-        for m in range(2):
-            y = first[:, WIDTH * m : WIDTH * (m + 1)]
-            activate(m, 0, WIDTH, y)
-            scatter(m, 0, WIDTH, y)
-        step(1, [0, 1], [(2, 0, WIDTH)])
-        step(1, [2, 3], [(3, 0, WIDTH)], [1, 2])
-        cuts = [WIDTH, 2 * WIDTH, 3 * WIDTH, 4 * WIDTH, S - KEPT]
-        waiting = [(m, lo, hi) for lo, hi in zip(cuts[:-1], cuts[1:]) for m in range(1, BLOCKS)]
-        for c in range(2, CHUNKS):
-            newest = (0, WIDTH * (c - 1), WIDTH * c)
-            older = waiting[2 * (c - 2) : 2 * (c - 1)]
-            if c < LAST:
-                step(c, [0, 1], older)
-                step(c, [2, 3], [newest], [m for m, lo, hi in waiting[2 * (c - 1) : 2 * c]] if c + 1 < LAST else [0])
-            else:
-                step(c, [0, 1], [older[0], newest])
-                step(c, [2, 3], [older[1]])
+        multiply(0, WIDTH, range(PASSES), range(BLOCKS))
+        W = WIDTH
+        early = S - KEPT
 
-        y = flat(LAST, PASSES - 1)[:, 0:WIDTH]
-        activate(0, S - WIDTH, S, y)
-        scatter(0, S - WIDTH, S, y)
+        def place(piece, y):
+            activate(*piece, y)
+            scatter(*piece, y)
+
+        for m in range(2):
+            place((m, 0, W), first[:, W * m : W * (m + 1)])
+        step(W, 2 * W, [0, 1], [(2, 0, W)])
+        step(W, 2 * W, [2, 3], [(3, 0, W)], 1)
+        place((1, W, 2 * W), flat(W, 2)[:, 0:W])
+        step(2 * W, 3 * W, [0, 1], [(2, W, 2 * W), (3, W, 2 * W)])
+        step(2 * W, 3 * W, [2, 3], [(0, W, 2 * W)], 1)
+        step(3 * W, MID, [0, 1], [(1, 2 * W, 3 * W), (2, 2 * W, 3 * W)])
+        step(3 * W, MID, [2, 3], [(0, 2 * W, 3 * W), (3, 2 * W, 3 * W)])
+        for a in range(PASSES):
+            step(MID, END, [a], [(a, 3 * W, MID)])
+        step(END, S, [0], [(0, MID, END)])
+        step(END, S, [1], [(1, MID, early)])
+        step(END, S, [2], [(2, MID, early)])
+        step(END, S, [3], [(3, MID, early)])
+
+        place((0, END, S), flat(END, 3)[:, BANK : 2 * BANK])
         nc.sync.dma_start(out[0:P, :], windows[0][:])
-        for m, home in ((1, flat(LAST, 1)), (2, flat(LAST - 1, 1)), (3, flat(LAST - 1, 3))):
-            activate(m, S - KEPT, S - BANK, home[:, 0 : KEPT - BANK])
-            activate(m, S - BANK, S, home[:, KEPT - BANK : KEPT])
-            scatter(m, S - KEPT, S, home[:, 0:KEPT])
+        for m in range(1, BLOCKS):
+            home = flat(END, m - 1)[:, LEAD : LEAD + KEPT]
+            activate(m, early, END, home[:, 0 : END - early])
+            activate(m, END, S, home[:, END - early : KEPT])
+            scatter(m, early, S, home)
             nc.sync.dma_start(out[P * m : P * (m + 1), :], windows[m][:])

@@ -138,14 +138,14 @@ def tile_list_hscat_silu_kernel(tc, x, w_words, w_scales, b, wgo, offs, out):
             for piece, y in zip(placed, ys):
                 scatter(*piece, y)
 
+        for q in range(4):
+            nc.scalar.dma_start(ws_sb[32 * q : 32 * q + 4, :, :].bitcast(I32), w_scales[:, 4 * q : 4 * q + 4, :].rearrange("a q n -> q a n").bitcast(I32))
         nc.gpsimd.memset(tiny[:], 0.0)
         nc.scalar.activation(tiny[:, 0:1], tiny[:, 1:2], SILU)
         load(0, WIDTH, 0)
         load(0, WIDTH, 1)
         load(0, WIDTH, 2)
         load(0, WIDTH, 3)
-        for q in range(4):
-            nc.sync.dma_start(ws_sb[32 * q : 32 * q + 4, :, :].bitcast(I32), w_scales[:, 4 * q : 4 * q + 4, :].rearrange("a q n -> q a n").bitcast(I32))
         nc.sync.dma_start(w_sb[:].bitcast(I32), w_view.bitcast(I32))
         with nc.allow_non_contiguous_dma(reason="512 bias values, one to a partition and block"):
             nc.sync.dma_start(b_sb[:], b.rearrange("(m p) -> p m", p=P))

@@ -26,6 +26,7 @@ MID = NARROW * WIDTH
 END = MID + BANK
 LEAD = 32
 KEPT = 704
+SPLIT = 96
 
 
 def tile_list_hscat_silu_kernel(tc, x, w_words, w_scales, b, wgo, offs, out):
@@ -42,7 +43,7 @@ def tile_list_hscat_silu_kernel(tc, x, w_words, w_scales, b, wgo, offs, out):
         b_sb = keep.tile([P, BLOCKS], F32, name="b_sb")
         tiny = keep.tile([P, 8], F32, name="tiny")
         wgo_sb = keep.tile([P, S], F32, name="wgo_sb")
-        first = keep.tile([P, 3 * WIDTH], F32, name="first")
+        first = keep.tile([P, 2 * WIDTH], F32, name="first")
         windows = [keep.tile([P, T], F32, name=f"window{m}") for m in range(BLOCKS - 1)]
         x_sb = keep.tile([P, K * S // P], F32, name="x_sb")
         raw = {}
@@ -69,20 +70,17 @@ def tile_list_hscat_silu_kernel(tc, x, w_words, w_scales, b, wgo, offs, out):
         def weave(dst, src, engine):
             engine(dst.rearrange("p (c i) t -> p c t i", i=4), src.rearrange("p t (c i) -> p c t i", i=4))
 
-        def interleave(lo, hi, passes, lead=0):
+        def interleave(lo, hi, passes, lead=0, ahead=None):
             cols = hi - lo
-            if (lo, passes[-1]) == (0, PASSES - 1):
-                t = keep.tile([P, 1, cols, 4], BF16, name="grouped_first", tag="late", align_bytes=64)
-            else:
-                t = group.tile([P, len(passes), cols, 4], BF16, name="grouped", align_bytes=64)
+            t = group.tile([P, len(passes), cols, 4], BF16, name="grouped", align_bytes=64)
             for i, a in enumerate(passes):
-                split = 96 if a == PASSES - 1 and lo < 1 * WIDTH else cols
-                cuts = [0, lead, split] if lead and a == passes[-1] else [0, split]
+                cuts = [0, lead, cols] if lead and (a == passes[-1] or ahead) else [0, cols]
                 for c0, c1 in zip(cuts[:-1], cuts[1:]):
                     weave(t[:, i, c0:c1, :], raw[lo, a][:, :, c0:c1], nc.scalar.copy)
-                if split < cols:
-                    weave(t[:, i, split:cols, :], raw[lo, a][:, :, split:cols], nc.vector.tensor_copy)
-            return t
+                if ahead and i == 0:
+                    at = start[lo, a] + lead
+                    place(ahead, x_sb[:, at - WIDTH : at])
+            return t[:]
 
         def quantize(grouped, lo, hi, passes):
             cols = hi - lo
@@ -91,7 +89,7 @@ def tile_list_hscat_silu_kernel(tc, x, w_words, w_scales, b, wgo, offs, out):
             for i, a in enumerate(passes):
                 codes[a] = words[:, i * cols : (i + 1) * cols]
                 scales[a] = plane[:, i * cols : (i + 1) * cols]
-            nc.vector.quantize_mx(out=words[:].bitcast(E4M3), scales=plane[:], in_=grouped[:].rearrange("p a c t -> p (a c t)"))
+            nc.vector.quantize_mx(out=words[:].bitcast(E4M3), scales=plane[:], in_=grouped.rearrange("p a c t -> p (a c t)"))
 
         def sums(m, lo, hi):
             if m == 0:
@@ -100,22 +98,19 @@ def tile_list_hscat_silu_kernel(tc, x, w_words, w_scales, b, wgo, offs, out):
                 return banks[m, c % 2][:, lo - starts[c] : hi - starts[c]]
             return banks[m, lo // BANK % 2 if lo >= WIDTH else 1][:, lo % BANK : lo % BANK + hi - lo]
 
-        def multiply(lo, hi, passes, blocks):
+        def multiply(lo, hi, blocks, later=range(PASSES)):
             for m in blocks:
-                size = hi - lo
-                n = BANK if size == hi - lo == BANK else P
-                for a in passes:
-                    words = w_sb[:, a, 2 * P * m : 2 * P * (m + 1)]
-                    for at in range(lo, hi, n):
-                        nc.tensor.matmul_mx(
-                            out=sums(m, at, at + n),
-                            lhsT=words.bitcast(E2M1),
-                            lhsT_scale=ws_sb[:, a, P * m : P * (m + 1)],
-                            rhs=codes[a][:, at - lo : at - lo + n].bitcast(E4M3),
-                            rhs_scale=scales[a][:, at - lo : at - lo + n],
-                            start=(a == 0 and at % size == 0),
-                            stop=(a == PASSES - 1 and (at + n) % size == 0),
-                        )
+                order = list(range(PASSES) if m == blocks[0] else later)
+                for a in order:
+                    nc.tensor.matmul_mx(
+                        out=sums(m, lo, hi),
+                        lhsT=w_sb[:, a, 2 * P * m : 2 * P * (m + 1)].bitcast(E2M1),
+                        lhsT_scale=ws_sb[:, a, P * m : P * (m + 1)],
+                        rhs=codes[a].bitcast(E4M3),
+                        rhs_scale=scales[a],
+                        start=(a == order[0]),
+                        stop=(a == order[-1]),
+                    )
 
         def activate(m, lo, hi, y):
             nc.scalar.activation(y, sums(m, lo, hi), SILU, bias=b_sb[:, m : m + 1])
@@ -126,15 +121,19 @@ def tile_list_hscat_silu_kernel(tc, x, w_words, w_scales, b, wgo, offs, out):
         def flat(lo, a):
             return x_sb[:, start[lo, a] : start[lo, a] + 2 * BANK]
 
-        def step(lo, hi, passes, placed, urgent=0):
-            grouped = interleave(lo, hi, passes, LEAD if placed else 0)
+        def place(piece, y):
+            activate(*piece, y)
+            scatter(*piece, y)
+
+        def step(lo, hi, passes, placed, urgent=0, ahead=None):
+            grouped = interleave(lo, hi, passes, LEAD if placed else 0, ahead)
             end = start[lo, passes[-1]] + LEAD
             ys = [x_sb[:, end - BANK * i - (to - at) : end - BANK * i] for i, (m, at, to) in enumerate(placed)]
             for piece, y in zip(placed, ys):
                 activate(*piece, y)
             quantize(grouped, lo, hi, passes)
             if passes[-1] == PASSES - 1:
-                multiply(lo, hi, range(PASSES), [(urgent + i) % BLOCKS for i in range(BLOCKS)])
+                multiply(lo, hi, [(urgent + i) % BLOCKS for i in range(BLOCKS)], [0, 1, 3, 2])
             for piece, y in zip(placed, ys):
                 scatter(*piece, y)
 
@@ -167,27 +166,31 @@ def tile_list_hscat_silu_kernel(tc, x, w_words, w_scales, b, wgo, offs, out):
         clear(nc.vector, 2, [0, 1023, T // 2])
         clear(nc.gpsimd, 2, [T // 2, T])
 
-        for passes in ([0, 1], [2], [3]):
-            quantize(interleave(0, WIDTH, passes), 0, WIDTH, passes)
+        quantize(interleave(0, WIDTH, [0, 1]), 0, WIDTH, [0, 1])
+        pair = keep.tile([P, 8 * WIDTH], BF16, name="pair", tag="late", align_bytes=64)[:].rearrange("p (a c t) -> p a c t", a=2, t=4)
+        both = x_sb[:, start[0, 2] : start[0, 2] + 8 * WIDTH].rearrange("p (a t c) -> p a t c", a=2, t=4)
+        weave(pair[:, 0, 4:WIDTH, :], both[:, 0, :, 4:WIDTH], nc.scalar.copy)
+        nc.scalar.copy(pair[:, :, 0:4, :].rearrange("p a c t -> p a t c"), both[:, :, :, 0:4])
+        weave(pair[:, 1, 4:SPLIT, :], both[:, 1, :, 4:SPLIT], nc.scalar.copy)
+        weave(pair[:, 1, SPLIT:WIDTH, :], both[:, 1, :, SPLIT:WIDTH], nc.vector.tensor_copy)
+        for i in range(2):
+            quantize(pair[:, i : i + 1], 0, WIDTH, [2 + i])
         windows.append(keep.tile([P, T], F32, name="window3", tag="late", align_bytes=64))
         clear(nc.gpsimd, 3, list(range(0, T + 1, 256)))
-        multiply(0, WIDTH, range(PASSES), range(BLOCKS))
+        multiply(0, WIDTH, list(range(BLOCKS)), [3, 0, 1, 2])
         W = WIDTH
         early = S - KEPT
-
-        def place(piece, y):
-            activate(*piece, y)
-            scatter(*piece, y)
 
         for m in range(2):
             place((m, 0, W), first[:, W * m : W * (m + 1)])
         step(W, 2 * W, [0, 1], [(2, 0, W)])
-        step(W, 2 * W, [2, 3], [(3, 0, W)], 1)
-        place((1, W, 2 * W), flat(W, 2)[:, 0:W])
-        step(2 * W, 3 * W, [0, 1], [(2, W, 2 * W), (3, W, 2 * W)])
-        step(2 * W, 3 * W, [2, 3], [(0, W, 2 * W)], 1)
-        step(3 * W, MID, [0, 1], [(1, 2 * W, 3 * W), (2, 2 * W, 3 * W)])
-        step(3 * W, MID, [2, 3], [(0, 2 * W, 3 * W), (3, 2 * W, 3 * W)])
+        step(W, 2 * W, [2], [])
+        step(W, 2 * W, [3], [(3, 0, W)], 1)
+        for lo in (2 * W, 3 * W):
+            place((1, lo - W, lo), flat(lo - W, 2)[:, 0:W])
+            step(lo, lo + W, [0, 1], [(3, lo - W, lo)], ahead=(2, lo - W, lo))
+            step(lo, lo + W, [2], [])
+            step(lo, lo + W, [3], [(0, lo - W, lo)], 1 if lo + W < MID else 0)
         for a in range(PASSES):
             step(MID, END, [a], [(a, 3 * W, MID)])
         step(END, S, [0], [(0, MID, END)])

@@ -18,6 +18,7 @@ P = 128
 PASSES = K // 512
 BLOCKS = M // P
 BANK = 512
+QUAD = 32
 FLOPS = 2 * K * M * S
 
 WIDTH = 256
@@ -27,23 +28,27 @@ END = MID + BANK
 LEAD = 32
 KEPT = 704
 SPLIT = 96
+RING = 4
+CLEAR = 256
 
 
 def tile_list_hscat_silu_kernel(tc, x, w_words, w_scales, b, wgo, offs, out):
     nc = tc.nc
     with ExitStack() as ctx:
         keep = ctx.enter_context(tc.tile_pool(name="keep", bufs=1))
-        group = ctx.enter_context(tc.tile_pool(name="group", bufs=4))
-        quant = ctx.enter_context(tc.tile_pool(name="quant", bufs=4))
+        group = ctx.enter_context(tc.tile_pool(name="group", bufs=RING))
+        quant = ctx.enter_context(tc.tile_pool(name="quant", bufs=RING))
         psum = ctx.enter_context(tc.psum_pool(name="psum", bufs=1))
 
         offs_sb = keep.tile([P, S // 16], U16, name="offs_sb")
         w_sb = keep.tile([P, PASSES, 2 * M], U8, name="w_sb", align_bytes=64)
+        zeroed = keep.tile([P, P + 8], F32, name="zeroed", tag="late", align_bytes=64)
+        b_rows = zeroed[:, 0:P]
+        tiny = zeroed[:, P : P + 8]
         ws_sb = keep.tile([P, PASSES, M], U8, name="ws_sb", align_bytes=64)
         b_sb = keep.tile([P, BLOCKS], F32, name="b_sb")
-        tiny = keep.tile([P, 8], F32, name="tiny")
         wgo_sb = keep.tile([P, S], F32, name="wgo_sb")
-        first = keep.tile([P, 2 * WIDTH], F32, name="first")
+        first = keep.tile([P, WIDTH], F32, name="first")
         windows = [keep.tile([P, T], F32, name=f"window{m}") for m in range(BLOCKS - 1)]
         x_sb = keep.tile([P, K * S // P], F32, name="x_sb")
         raw = {}
@@ -51,6 +56,10 @@ def tile_list_hscat_silu_kernel(tc, x, w_words, w_scales, b, wgo, offs, out):
         banks = {(m, h): psum.tile([P, BANK], F32, name=f"bank{m}{h}") for m in range(BLOCKS) for h in range(2)}
         w_view = w_words.rearrange("a p c -> p a c")
 
+        late_pair = keep.tile([P, 8 * WIDTH], BF16, name="late_pair", tag="ramp", align_bytes=64)
+        pair = late_pair[:].rearrange("p (a c t) -> p a c t", a=2, t=4)
+        b_turned = late_pair[:, 0 : 2 * P].bitcast(F32)
+        b_early = b_turned[:, 0:P:QUAD]
         codes = {}
         scales = {}
 
@@ -70,20 +79,16 @@ def tile_list_hscat_silu_kernel(tc, x, w_words, w_scales, b, wgo, offs, out):
         def weave(dst, src, engine):
             engine(dst.rearrange("p (c i) t -> p c t i", i=4), src.rearrange("p t (c i) -> p c t i", i=4))
 
-        def interleave(lo, hi, passes, lead=0, ahead=None):
+        def interleave(lo, hi, passes, lead=0):
             cols = hi - lo
-            t = group.tile([P, len(passes), cols, 4], BF16, name="grouped", align_bytes=64)
+            t = group.tile([P, len(passes) * 4 * cols], BF16, name="grouped", align_bytes=64)[:].rearrange("p (a c t) -> p a c t", a=len(passes), t=4)
             for i, a in enumerate(passes):
-                cuts = [0, lead, cols] if lead and (a == passes[-1] or ahead) else [0, cols]
+                cuts = [0, lead, cols] if lead and a == passes[-1] else [0, cols]
                 for c0, c1 in zip(cuts[:-1], cuts[1:]):
                     weave(t[:, i, c0:c1, :], raw[lo, a][:, :, c0:c1], nc.scalar.copy)
-                if ahead and i == 0:
-                    at = start[lo, a] + lead
-                    place(ahead, x_sb[:, at - WIDTH : at])
-            return t[:]
+            return t
 
-        def quantize(grouped, lo, hi, passes):
-            cols = hi - lo
+        def quantize(grouped, cols, passes):
             words = quant.tile([P, len(passes) * cols], U32, name="words", align_bytes=64)
             plane = quant.tile([P, len(passes) * cols], U8, name="plane", align_bytes=64)
             for i, a in enumerate(passes):
@@ -113,7 +118,8 @@ def tile_list_hscat_silu_kernel(tc, x, w_words, w_scales, b, wgo, offs, out):
                     )
 
         def activate(m, lo, hi, y):
-            nc.scalar.activation(y, sums(m, lo, hi), SILU, bias=b_sb[:, m : m + 1])
+            bias = b_early if (m, lo) == (0, 0) else b_sb
+            nc.scalar.activation(y, sums(m, lo, hi), SILU, bias=bias[:, m : m + 1])
 
         def scatter(m, lo, hi, y):
             nc.vector.tensor_tensor(windows[m][:].indirect(offs_sb[:, lo // 16 : hi // 16]), y, wgo_sb[:, lo:hi], MULT)
@@ -125,29 +131,27 @@ def tile_list_hscat_silu_kernel(tc, x, w_words, w_scales, b, wgo, offs, out):
             activate(*piece, y)
             scatter(*piece, y)
 
-        def step(lo, hi, passes, placed, urgent=0, ahead=None):
-            grouped = interleave(lo, hi, passes, LEAD if placed else 0, ahead)
+        def step(lo, hi, passes, placed, urgent=0):
+            grouped = interleave(lo, hi, passes, LEAD)
             end = start[lo, passes[-1]] + LEAD
             ys = [x_sb[:, end - BANK * i - (to - at) : end - BANK * i] for i, (m, at, to) in enumerate(placed)]
             for piece, y in zip(placed, ys):
                 activate(*piece, y)
-            quantize(grouped, lo, hi, passes)
+            quantize(grouped, hi - lo, passes)
             if passes[-1] == PASSES - 1:
-                multiply(lo, hi, [(urgent + i) % BLOCKS for i in range(BLOCKS)], [0, 1, 3, 2])
+                multiply(lo, hi, [(urgent + i) % BLOCKS for i in range(BLOCKS)])
             for piece, y in zip(placed, ys):
                 scatter(*piece, y)
 
         for q in range(4):
-            nc.scalar.dma_start(ws_sb[32 * q : 32 * q + 4, :, :].bitcast(I32), w_scales[:, 4 * q : 4 * q + 4, :].rearrange("a q n -> q a n").bitcast(I32))
-        nc.gpsimd.memset(tiny[:], 0.0)
+            nc.scalar.dma_start(ws_sb[QUAD * q : QUAD * q + 4, :, :].bitcast(I32), w_scales[:, 4 * q : 4 * q + 4, :].rearrange("a q n -> q a n").bitcast(I32))
+        nc.gpsimd.memset(zeroed[:], 0.0)
         nc.scalar.activation(tiny[:, 0:1], tiny[:, 1:2], SILU)
-        load(0, WIDTH, 0)
-        load(0, WIDTH, 1)
-        load(0, WIDTH, 2)
-        load(0, WIDTH, 3)
+
+        for a in range(PASSES):
+            load(0, WIDTH, a)
         nc.sync.dma_start(w_sb[:].bitcast(I32), w_view.bitcast(I32))
-        with nc.allow_non_contiguous_dma(reason="512 bias values, one to a partition and block"):
-            nc.sync.dma_start(b_sb[:], b.rearrange("(m p) -> p m", p=P))
+        nc.sync.dma_start(zeroed[0:P:QUAD, 0:P].rearrange("q (m c) -> q m c", c=QUAD), b.rearrange("(m q c) -> q m c", m=BLOCKS, c=QUAD))
         nc.sync.dma_start(offs_sb[:], offs)
         load_wgo(0, WIDTH)
         for lo in range(WIDTH, MID, WIDTH):
@@ -161,44 +165,54 @@ def tile_list_hscat_silu_kernel(tc, x, w_words, w_scales, b, wgo, offs, out):
                 if a == 0:
                     load_wgo(lo - (WIDTH if lo == MID else BANK), lo)
         load_wgo(END, S)
-        clear(nc.vector, 0, [0, 2047, T])
+
+        clear(nc.vector, 0, [0, T // 2 - 1, T])
         clear(nc.gpsimd, 1, [0, T])
-        clear(nc.vector, 2, [0, 1023, T // 2])
+        clear(nc.vector, 2, [0, T // 4 - 1, T // 2])
         clear(nc.gpsimd, 2, [T // 2, T])
 
-        quantize(interleave(0, WIDTH, [0, 1]), 0, WIDTH, [0, 1])
-        pair = keep.tile([P, 8 * WIDTH], BF16, name="pair", tag="late", align_bytes=64)[:].rearrange("p (a c t) -> p a c t", a=2, t=4)
-        both = x_sb[:, start[0, 2] : start[0, 2] + 8 * WIDTH].rearrange("p (a t c) -> p a t c", a=2, t=4)
-        weave(pair[:, 0, 4:WIDTH, :], both[:, 0, :, 4:WIDTH], nc.scalar.copy)
+        W = WIDTH
+        quantize(interleave(0, W, [0, 1]), W, [0, 1])
+        both = x_sb[:, start[0, 2] : start[0, 2] + 8 * W].rearrange("p (a t c) -> p a t c", a=2, t=4)
+        weave(pair[:, 0, 4:W, :], both[:, 0, :, 4:W], nc.scalar.copy)
         nc.scalar.copy(pair[:, :, 0:4, :].rearrange("p a c t -> p a t c"), both[:, :, :, 0:4])
         weave(pair[:, 1, 4:SPLIT, :], both[:, 1, :, 4:SPLIT], nc.scalar.copy)
-        weave(pair[:, 1, SPLIT:WIDTH, :], both[:, 1, :, SPLIT:WIDTH], nc.vector.tensor_copy)
+        weave(pair[:, 1, SPLIT:W, :], both[:, 1, :, SPLIT:W], nc.vector.tensor_copy)
         for i in range(2):
-            quantize(pair[:, i : i + 1], 0, WIDTH, [2 + i])
-        windows.append(keep.tile([P, T], F32, name="window3", tag="late", align_bytes=64))
-        clear(nc.gpsimd, 3, list(range(0, T + 1, 256)))
-        multiply(0, WIDTH, list(range(BLOCKS)), [3, 0, 1, 2])
-        W = WIDTH
-        early = S - KEPT
+            quantize(pair[:, i : i + 1], W, [2 + i])
+        nc.vector.transpose(b_turned, b_rows)
 
-        for m in range(2):
-            place((m, 0, W), first[:, W * m : W * (m + 1)])
-        step(W, 2 * W, [0, 1], [(2, 0, W)])
-        step(W, 2 * W, [2], [])
-        step(W, 2 * W, [3], [(3, 0, W)], 1)
-        for lo in (2 * W, 3 * W):
-            place((1, lo - W, lo), flat(lo - W, 2)[:, 0:W])
-            step(lo, lo + W, [0, 1], [(3, lo - W, lo)], ahead=(2, lo - W, lo))
-            step(lo, lo + W, [2], [])
-            step(lo, lo + W, [3], [(0, lo - W, lo)], 1 if lo + W < MID else 0)
+        windows.append(keep.tile([P, T], F32, name="window3", tag="late", align_bytes=64))
+        clear(nc.gpsimd, 3, list(range(2 * CLEAR, T + 1, CLEAR)))
+        clear(nc.vector, 3, [0, CLEAR - 1, 2 * CLEAR])
+        multiply(0, W, list(range(BLOCKS)), [3, 0, 1, 2])
+
+        nc.scalar.copy(b_sb[:], b_early)
+        place((0, 0, W), first[:])
+        next_pair = keep.tile([P, 2, W, 4], BF16, name="next_pair", tag="ramp", align_bytes=64)
+        ys = [x_sb[:, start[W, a] + LEAD - W : start[W, a] + LEAD] for a in range(2)]
+        for a in range(2):
+            for c0, c1 in ((0, LEAD), (LEAD, W)):
+                weave(next_pair[:, a, c0:c1, :], raw[W, a][:, :, c0:c1], nc.scalar.copy)
+            activate(a + 1, 0, W, ys[a])
+        scatter(1, 0, W, ys[0])
+        quantize(next_pair[:], W, [0, 1])
+        scatter(2, 0, W, ys[1])
+
+        step(W, 2 * W, [2, 3], [(3, 0, W)], 1)
+        place((1, W, 2 * W), flat(W, 2)[:, 0:W])
+        step(2 * W, 3 * W, [0, 1], [(2, W, 2 * W), (3, W, 2 * W)])
+        step(2 * W, 3 * W, [2, 3], [(0, W, 2 * W)], 1)
+        step(3 * W, MID, [0, 1], [(1, 2 * W, 3 * W), (2, 2 * W, 3 * W)])
+        step(3 * W, MID, [2, 3], [(0, 2 * W, 3 * W), (3, 2 * W, 3 * W)])
+
+        early = S - KEPT
         for a in range(PASSES):
             step(MID, END, [a], [(a, 3 * W, MID)])
-        step(END, S, [0], [(0, MID, END)])
-        step(END, S, [1], [(1, MID, early)])
-        step(END, S, [2], [(2, MID, early)])
-        step(END, S, [3], [(3, MID, early)])
+        for a in range(PASSES):
+            step(END, S, [a], [(a, MID, early if a else END)])
 
-        place((0, END, S), flat(END, 3)[:, BANK : 2 * BANK])
+        place((0, END, S), flat(END, PASSES - 1)[:, BANK : 2 * BANK])
         nc.sync.dma_start(out[0:P, :], windows[0][:])
         for m in range(1, BLOCKS):
             home = flat(END, m - 1)[:, LEAD : LEAD + KEPT]

@@ -69,6 +69,14 @@ def tile_list_hscat_silu_kernel(tc, x, w_words, w_scales, b, wgo, offs, out):
             raw[lo, a] = x_sb[:, at : at + 4 * (hi - lo)].rearrange("p (i j) -> p i j", i=4)
             nc.sync.dma_start(raw[lo, a], x[512 * a : 512 * a + 512, lo:hi].rearrange("(p i) j -> p i j", i=4))
 
+        def load_pair(lo, hi):
+            at = sum(4 * t.shape[2] for t in raw.values())
+            both = x_sb[:, at : at + 8 * (hi - lo)].rearrange("p (i a j) -> p i a j", i=4, a=2)
+            for a in range(2):
+                start[lo, a] = at + 4 * a * (hi - lo)
+                raw[lo, a] = both[:, :, a, :]
+            nc.sync.dma_start(both, x[0:1024, lo:hi].rearrange("(a p i) j -> p i a j", a=2, i=4))
+
         def load_wgo(lo, hi):
             nc.sync.dma_start(wgo_sb[:, lo:hi], wgo[:, lo:hi])
 
@@ -148,7 +156,8 @@ def tile_list_hscat_silu_kernel(tc, x, w_words, w_scales, b, wgo, offs, out):
         nc.gpsimd.memset(zeroed[:], 0.0)
         nc.scalar.activation(tiny[:, 0:1], tiny[:, 1:2], SILU)
 
-        for a in range(PASSES):
+        load_pair(0, WIDTH)
+        for a in range(2, PASSES):
             load(0, WIDTH, a)
         nc.sync.dma_start(w_sb[:].bitcast(I32), w_view.bitcast(I32))
         nc.sync.dma_start(zeroed[0:P:QUAD, 0:P].rearrange("q (m c) -> q m c", c=QUAD), b.rearrange("(m q c) -> q m c", m=BLOCKS, c=QUAD))

from contextlib import ExitStack

import concourse.mybir as mybir

F32 = mybir.dt.float32
BF16 = mybir.dt.bfloat16
I32 = mybir.dt.int32
U32 = mybir.dt.uint32
U16 = mybir.dt.uint16
U8 = mybir.dt.uint8
E4M3 = mybir.dt.float8_e4m3fn_x4
E2M1 = mybir.dt.float4_e2m1fn_x4
SILU = mybir.ActivationFunctionType.Silu
MULT = mybir.AluOpType.mult

K, M, T, S = 2048, 512, 4096, 2048
P = 128
PASSES = K // 512
BLOCKS = M // P
BANK = 512
QUAD = 32
FLOPS = 2 * K * M * S

WIDTH = 256
NARROW = 4
MID = NARROW * WIDTH
END = MID + BANK
LEAD = 32
KEPT = 704
SPLIT = 96
RING = 4
CLEAR = 256


def tile_list_hscat_silu_kernel(tc, x, w_words, w_scales, b, wgo, offs, out):
    nc = tc.nc
    with ExitStack() as ctx:
        keep = ctx.enter_context(tc.tile_pool(name="keep", bufs=1))
        group = ctx.enter_context(tc.tile_pool(name="group", bufs=RING))
        quant = ctx.enter_context(tc.tile_pool(name="quant", bufs=RING))
        psum = ctx.enter_context(tc.psum_pool(name="psum", bufs=1))

        offs_sb = keep.tile([P, S // 16], U16, name="offs_sb")
        w_sb = keep.tile([P, PASSES, 2 * M], U8, name="w_sb", align_bytes=64)
        zeroed = keep.tile([P, P + 8], F32, name="zeroed", tag="late", align_bytes=64)
        b_rows = zeroed[:, 0:P]
        tiny = zeroed[:, P : P + 8]
        ws_sb = keep.tile([P, PASSES, M], U8, name="ws_sb", align_bytes=64)
        b_sb = keep.tile([P, BLOCKS], F32, name="b_sb")
        wgo_sb = keep.tile([P, S], F32, name="wgo_sb")
        first = keep.tile([P, WIDTH], F32, name="first")
        windows = [keep.tile([P, T], F32, name=f"window{m}") for m in range(BLOCKS - 1)]
        x_sb = keep.tile([P, K * S // P], F32, name="x_sb")
        raw = {}
        start = {}
        banks = {(m, h): psum.tile([P, BANK], F32, name=f"bank{m}{h}") for m in range(BLOCKS) for h in range(2)}
        w_view = w_words.rearrange("a p c -> p a c")

        late_pair = keep.tile([P, 8 * WIDTH], BF16, name="late_pair", tag="ramp", align_bytes=64)
        pair = late_pair[:].rearrange("p (a c t) -> p a c t", a=2, t=4)
        b_turned = late_pair[:, 0 : 2 * P].bitcast(F32)
        b_early = b_turned[:, 0:P:QUAD]
        codes = {}
        scales = {}

        def load(lo, hi, a):
            at = sum(4 * t.shape[2] for t in raw.values())
            start[lo, a] = at
            raw[lo, a] = x_sb[:, at : at + 4 * (hi - lo)].rearrange("p (i j) -> p i j", i=4)
            nc.sync.dma_start(raw[lo, a], x[512 * a : 512 * a + 512, lo:hi].rearrange("(p i) j -> p i j", i=4))

        def load_pair(lo, hi):
            at = sum(4 * t.shape[2] for t in raw.values())
            both = x_sb[:, at : at + 8 * (hi - lo)].rearrange("p (i a j) -> p i a j", i=4, a=2)
            for a in range(2):
                start[lo, a] = at + 4 * a * (hi - lo)
                raw[lo, a] = both[:, :, a, :]
            nc.sync.dma_start(both, x[0:1024, lo:hi].rearrange("(a p i) j -> p i a j", a=2, i=4))

        def load_wgo(lo, hi):
            nc.sync.dma_start(wgo_sb[:, lo:hi], wgo[:, lo:hi])

        def clear(engine, m, cuts):
            for lo, hi in zip(cuts[:-1], cuts[1:]):
                engine.memset(windows[m][:, lo:hi], 0.0)

        def weave(dst, src, engine):
            engine(dst.rearrange("p (c i) t -> p c t i", i=4), src.rearrange("p t (c i) -> p c t i", i=4))

        def interleave(lo, hi, passes, lead=0):
            cols = hi - lo
            t = group.tile([P, len(passes) * 4 * cols], BF16, name="grouped", align_bytes=64)[:].rearrange("p (a c t) -> p a c t", a=len(passes), t=4)
            for i, a in enumerate(passes):
                cuts = [0, lead, cols] if lead and a == passes[-1] else [0, cols]
                for c0, c1 in zip(cuts[:-1], cuts[1:]):
                    weave(t[:, i, c0:c1, :], raw[lo, a][:, :, c0:c1], nc.scalar.copy)
            return t

        def quantize(grouped, cols, passes):
            words = quant.tile([P, len(passes) * cols], U32, name="words", align_bytes=64)
            plane = quant.tile([P, len(passes) * cols], U8, name="plane", align_bytes=64)
            for i, a in enumerate(passes):
                codes[a] = words[:, i * cols : (i + 1) * cols]
                scales[a] = plane[:, i * cols : (i + 1) * cols]
            nc.vector.quantize_mx(out=words[:].bitcast(E4M3), scales=plane[:], in_=grouped.rearrange("p a c t -> p (a c t)"))

        def sums(m, lo, hi):
            if m == 0:
                starts = [WIDTH * c for c in range(NARROW)] + [MID, END]
                c = max(i for i, at in enumerate(starts) if at <= lo)
                return banks[m, c % 2][:, lo - starts[c] : hi - starts[c]]
            return banks[m, lo // BANK % 2 if lo >= WIDTH else 1][:, lo % BANK : lo % BANK + hi - lo]

        def multiply(lo, hi, blocks, later=range(PASSES)):
            for m in blocks:
                order = list(range(PASSES) if m == blocks[0] else later)
                for a in order:
                    nc.tensor.matmul_mx(
                        out=sums(m, lo, hi),
                        lhsT=w_sb[:, a, 2 * P * m : 2 * P * (m + 1)].bitcast(E2M1),
                        lhsT_scale=ws_sb[:, a, P * m : P * (m + 1)],
                        rhs=codes[a].bitcast(E4M3),
                        rhs_scale=scales[a],
                        start=(a == order[0]),
                        stop=(a == order[-1]),
                    )

        def activate(m, lo, hi, y):
            bias = b_early if (m, lo) == (0, 0) else b_sb
            nc.scalar.activation(y, sums(m, lo, hi), SILU, bias=bias[:, m : m + 1])

        def scatter(m, lo, hi, y):
            nc.vector.tensor_tensor(windows[m][:].indirect(offs_sb[:, lo // 16 : hi // 16]), y, wgo_sb[:, lo:hi], MULT)

        def flat(lo, a):
            return x_sb[:, start[lo, a] : start[lo, a] + 2 * BANK]

        def place(piece, y):
            activate(*piece, y)
            scatter(*piece, y)

        def step(lo, hi, passes, placed, urgent=0):
            grouped = interleave(lo, hi, passes, LEAD)
            end = start[lo, passes[-1]] + LEAD
            ys = [x_sb[:, end - BANK * i - (to - at) : end - BANK * i] for i, (m, at, to) in enumerate(placed)]
            for piece, y in zip(placed, ys):
                activate(*piece, y)
            quantize(grouped, hi - lo, passes)
            if passes[-1] == PASSES - 1:
                multiply(lo, hi, [(urgent + i) % BLOCKS for i in range(BLOCKS)])
            for piece, y in zip(placed, ys):
                scatter(*piece, y)

        for q in range(4):
            nc.scalar.dma_start(ws_sb[QUAD * q : QUAD * q + 4, :, :].bitcast(I32), w_scales[:, 4 * q : 4 * q + 4, :].rearrange("a q n -> q a n").bitcast(I32))
        nc.gpsimd.memset(zeroed[:], 0.0)
        nc.scalar.activation(tiny[:, 0:1], tiny[:, 1:2], SILU)

        load_pair(0, WIDTH)
        for a in range(2, PASSES):
            load(0, WIDTH, a)
        nc.sync.dma_start(w_sb[:].bitcast(I32), w_view.bitcast(I32))
        nc.sync.dma_start(zeroed[0:P:QUAD, 0:P].rearrange("q (m c) -> q m c", c=QUAD), b.rearrange("(m q c) -> q m c", m=BLOCKS, c=QUAD))
        nc.sync.dma_start(offs_sb[:], offs)
        load_wgo(0, WIDTH)
        for lo in range(WIDTH, MID, WIDTH):
            for a in range(PASSES):
                load(lo, lo + WIDTH, a)
                if (lo, a) == (2 * WIDTH, 0):
                    load_wgo(WIDTH, 3 * WIDTH)
        for lo in (MID, END):
            for a in range(PASSES):
                load(lo, lo + BANK, a)
                if a == 0:
                    load_wgo(lo - (WIDTH if lo == MID else BANK), lo)
        load_wgo(END, S)

        clear(nc.vector, 0, [0, T // 2 - 1, T])
        clear(nc.gpsimd, 1, [0, T])
        clear(nc.vector, 2, [0, T // 4 - 1, T // 2])
        clear(nc.gpsimd, 2, [T // 2, T])

        W = WIDTH
        quantize(interleave(0, W, [0, 1]), W, [0, 1])
        both = x_sb[:, start[0, 2] : start[0, 2] + 8 * W].rearrange("p (a t c) -> p a t c", a=2, t=4)
        weave(pair[:, 0, 4:W, :], both[:, 0, :, 4:W], nc.scalar.copy)
        nc.scalar.copy(pair[:, :, 0:4, :].rearrange("p a c t -> p a t c"), both[:, :, :, 0:4])
        weave(pair[:, 1, 4:SPLIT, :], both[:, 1, :, 4:SPLIT], nc.scalar.copy)
        weave(pair[:, 1, SPLIT:W, :], both[:, 1, :, SPLIT:W], nc.vector.tensor_copy)
        for i in range(2):
            quantize(pair[:, i : i + 1], W, [2 + i])
        nc.vector.transpose(b_turned, b_rows)

        windows.append(keep.tile([P, T], F32, name="window3", tag="late", align_bytes=64))
        clear(nc.gpsimd, 3, list(range(2 * CLEAR, T + 1, CLEAR)))
        clear(nc.vector, 3, [0, CLEAR - 1, 2 * CLEAR])
        multiply(0, W, list(range(BLOCKS)), [3, 0, 1, 2])

        nc.scalar.copy(b_sb[:], b_early)
        place((0, 0, W), first[:])
        next_pair = keep.tile([P, 2, W, 4], BF16, name="next_pair", tag="ramp", align_bytes=64)
        ys = [x_sb[:, start[W, a] + LEAD - W : start[W, a] + LEAD] for a in range(2)]
        for a in range(2):
            for c0, c1 in ((0, LEAD), (LEAD, W)):
                weave(next_pair[:, a, c0:c1, :], raw[W, a][:, :, c0:c1], nc.scalar.copy)
            activate(a + 1, 0, W, ys[a])
        scatter(1, 0, W, ys[0])
        quantize(next_pair[:], W, [0, 1])
        scatter(2, 0, W, ys[1])

        step(W, 2 * W, [2, 3], [(3, 0, W)], 1)
        place((1, W, 2 * W), flat(W, 2)[:, 0:W])
        step(2 * W, 3 * W, [0, 1], [(2, W, 2 * W), (3, W, 2 * W)])
        step(2 * W, 3 * W, [2, 3], [(0, W, 2 * W)], 1)
        step(3 * W, MID, [0, 1], [(1, 2 * W, 3 * W), (2, 2 * W, 3 * W)])
        step(3 * W, MID, [2, 3], [(0, 2 * W, 3 * W), (3, 2 * W, 3 * W)])

        early = S - KEPT
        for a in range(PASSES):
            step(MID, END, [a], [(a, 3 * W, MID)])
        for a in range(PASSES):
            step(END, S, [a], [(a, MID, early if a else END)])

        place((0, END, S), flat(END, PASSES - 1)[:, BANK : 2 * BANK])
        nc.sync.dma_start(out[0:P, :], windows[0][:])
        for m in range(1, BLOCKS):
            home = flat(END, m - 1)[:, LEAD : LEAD + KEPT]
            activate(m, early, END, home[:, 0 : END - early])
            activate(m, END, S, home[:, END - early : KEPT])
            scatter(m, early, S, home)
            nc.sync.dma_start(out[P * m : P * (m + 1), :], windows[m][:])
